import numpy as np
import ml_dtypes


def mxq(x, axis, fmt="e4m3"):
    dtype, down = {"e4m3": (ml_dtypes.float8_e4m3fn, 7), "e5m2": (ml_dtypes.float8_e5m2, 14)}[fmt]
    v = np.moveaxis(np.asarray(x, np.float32).astype(ml_dtypes.bfloat16).astype(np.float64), axis, -1)
    blocks = v.reshape(v.shape[:-1] + (-1, 32))
    amax = np.abs(blocks).max(-1, keepdims=True)
    byte = np.maximum(np.where(amax > 0, np.frexp(amax)[1] - 1 + 127, 0) - down, 1)
    scale = np.exp2(byte - 127.0)
    codes = (blocks / scale).astype(np.float32).astype(dtype).astype(np.float64)
    return np.moveaxis((codes * scale).reshape(v.shape), -1, axis)


WIDE = False


def mx_kscale(k):
    if not WIDE:
        return np.ones(k)
    levels = np.array([10, -10, 5, -5, 0])
    if k % 512:
        return np.exp2(np.random.permutation(np.resize(levels, k // 32))).repeat(32)
    a = np.empty((k // 512, 16))
    for p in range(k // 512):
        a[p, :8] = np.random.permutation(np.resize(levels, 8))
        for g in range(8):
            far = levels[np.abs(levels - a[p, g]) >= 10]
            a[p, g + 8] = far[np.random.randint(len(far))]
    return np.exp2(a.ravel()).repeat(32)


def f64(x):
    return np.asarray(x).astype(np.float64)


def striped(idx):
    return np.tile(np.asarray(idx).reshape(-1, 16).T, (8, 1)).astype(np.uint16)


def unstriped(offs):
    return offs[:16].T.reshape(-1).astype(np.int64)


E2M1 = np.array([0.0, 0.5, 1.0, 1.5, 2.0, 3.0, 4.0, 6.0, -0.0, -0.5, -1.0, -1.5, -2.0, -3.0, -4.0, -6.0])


def pack_weight(w, fmt):
    k, n = w.shape
    w = f64(np.asarray(w, np.float32).astype(ml_dtypes.bfloat16)).reshape(k // 32, 32, n)
    amax = np.abs(w).max(1)
    if fmt == "e4m3":
        byte = np.frexp(amax)[1] - 1 + 127 - 7
    else:
        mant, ex = np.frexp(amax / 6.0)
        byte = np.where(mant > 0.5, ex, ex - 1) + 127
    byte = np.clip(np.where(amax > 0, byte, 1), 1, 254)
    scaled = (w * np.exp2(127.0 - byte)[:, None, :]).reshape(k, n).astype(np.float32)
    by_word = np.ascontiguousarray(scaled.reshape(k // 512, 128, 4, n).transpose(0, 1, 3, 2))
    if fmt == "e4m3":
        words = by_word.astype(ml_dtypes.float8_e4m3fn).view(np.uint8)
    else:
        c = by_word.astype(ml_dtypes.float4_e2m1fn).view(np.uint8) & 0xF
        words = (c[..., 0::2] | (c[..., 1::2] << 4)).reshape(k // 512, 128, 2 * n)
    return np.ascontiguousarray(words), np.ascontiguousarray(byte.astype(np.uint8).reshape(k // 512, 16, n))


def unpack_weight(words, scales, fmt):
    g, _, n = scales.shape
    words = np.ascontiguousarray(words).reshape(g, 128, n, -1)
    if fmt == "e4m3":
        vals = words.view(ml_dtypes.float8_e4m3fn).astype(np.float64)
    else:
        nib = np.empty((g, 128, n, 4), np.uint8)
        nib[..., 0::2] = words & 0xF
        nib[..., 1::2] = words >> 4
        vals = E2M1[nib]
    vals = vals * np.repeat(np.exp2(scales.astype(np.float64) - 127.0), 8, axis=1)[..., None]
    return vals.transpose(0, 1, 3, 2).reshape(g * 512, n)


D, T, G, U, I, Q = 512, 2048, 256, 1024, 1024, 128


def setup_inputs():
    n = np.random.standard_normal
    idx = np.random.permutation(T)[:G]
    idx2 = np.random.randint(0, U, I)
    fd = mx_kscale(D)
    emitp = pack_weight(n((D, T)) / fd[:, None], "e4m3")
    return {
        "obs": (n((D, Q)) * 1.0 / np.sqrt(D) * fd[:, None]).astype(np.float32),
        "emit_words": emitp[0],
        "emit_scales": emitp[1],
        "cum": (1.0 * n((Q, U))).astype(np.float32),
        "step": (0.5 * n((1, I))).astype(np.float32),
        "offs": striped(idx),
        "offs2": striped(idx2),
    }


def reference(obs, emit_words, emit_scales, cum, step, offs, offs2):
    idx = unstriped(offs)
    idx2 = unstriped(offs2)
    emitu = unpack_weight(emit_words, emit_scales, "e4m3")
    s = f64(cum)[:, idx2] + f64(step)
    best = s.reshape(Q, G, I // G).max(axis=2)
    obsq = mxq(f64(obs), 0, "e4m3")
    emitidxg = emitu[:, idx]
    a = obsq.T @ emitidxg
    y = best + a
    return y

@@ -1,0 +1,119 @@
+from contextlib import ExitStack
+
+import concourse.mybir as mybir
+from concourse.masks import make_identity
+
+D, T, G, U, I, Q = 512, 2048, 256, 1024, 1024, 128
+FLOPS = 2 * D * Q * G
+
+F32 = mybir.dt.float32
+BF16 = mybir.dt.bfloat16
+I32 = mybir.dt.int32
+U32 = mybir.dt.uint32
+U16 = mybir.dt.uint16
+U8 = mybir.dt.uint8
+FP8X4 = mybir.dt.float8_e4m3fn_x4
+ADD = mybir.AluOpType.add
+MAX = mybir.AluOpType.max
+
+P = 128
+R = 4
+RUN = 256
+PIECES = ((0, 1), (1, 2), (2, 4))
+HG = G // 2
+
+
+def tile_attend_viterbistep_kernel(tc, obs, emit_words, emit_scales, cum, step, offs, offs2, out):
+    nc = tc.nc
+    with ExitStack() as ctx:
+        sb = ctx.enter_context(tc.tile_pool(name="sb", bufs=1))
+        ps = ctx.enter_context(tc.psum_pool(name="ps", bufs=1))
+
+        cum_sb = sb.tile([P, U], F32, name="cum_sb")
+        offs2_sb = sb.tile([P, I // 16], U16, name="offs2_sb")
+        offs_sb = sb.tile([P, G // 16], U16, name="offs_sb")
+        obs_sb = sb.tile([P, 4, Q], F32, name="obs_sb")
+        words = sb.tile([P, T], I32, name="words", tag="words")
+        scales = sb.tile([P, T], U8, name="scales", tag="scales")
+        step_a = sb.tile([P, 1, 8], F32, name="step_a")
+        step_b = sb.tile([P, 3, 8], F32, name="step_b")
+        ident = sb.tile([P, P], F32, name="ident")
+
+        nc.vector.memset(scales[:].bitcast(I32), 0)
+        nc.scalar.dma_start(out=step_a[:, :, 0:2], in_=step[0, 0:RUN].rearrange("(h p c) -> p h c", h=1, c=2))
+        nc.scalar.dma_start(out=step_b[:, :, 0:2], in_=step[0, RUN:I].rearrange("(h p c) -> p h c", h=3, c=2))
+        nc.sync.dma_start(out=cum_sb[:], in_=cum)
+        nc.sync.dma_start(offs2_sb[:], offs2)
+        nc.sync.dma_start(out=obs_sb[:], in_=obs.rearrange("(p j) q -> p j q", j=4))
+        nc.sync.dma_start(out=words[:], in_=emit_words[0].rearrange("p n t -> p (n t)").bitcast(I32))
+        nc.sync.dma_start(offs_sb[:], offs)
+        for quad in range(4):
+            nc.sync.dma_start(
+                out=scales[32 * quad : 32 * quad + 4, :].bitcast(I32),
+                in_=emit_scales[0, 4 * quad : 4 * quad + 4, :].bitcast(I32),
+            )
+        make_identity(nc, ident[:])
+
+        step_cols = [step_a[:, 0, :], step_b[:, 0, :], step_b[:, 1, :], step_b[:, 2, :]]
+        s = sb.tile([P, I], F32, name="s")
+        rows = []
+        for lo, hi in PIECES:
+            n = hi - lo
+            spread = ps.tile([P, n, 2, P], F32, name="spread%d" % lo)
+            for h in range(n):
+                for c in range(2):
+                    nc.tensor.transpose(spread[:, h, c, :], step_cols[lo + h][:, c : c + 1].to_broadcast([P, P]), ident[:])
+            row = sb.tile([P, n, P, 2], F32, name="step_row%d" % lo)
+            nc.scalar.copy(row[:], spread[:].rearrange("q h c p -> q h p c"))
+            rows.append(row)
+
+        obs_bf = sb.tile([P, Q, 4], BF16, name="obs_bf", align_bytes=64)
+        nc.scalar.copy(
+            obs_bf[:].rearrange("p (c i) j -> p c j i", i=4),
+            obs_sb[:].rearrange("p j (c i) -> p c j i", i=4),
+        )
+
+        for (lo, hi), row in zip(PIECES, rows):
+            nc.vector.tensor_tensor(
+                s[:, lo * RUN : hi * RUN],
+                cum_sb[:].indirect(offs2_sb[:, lo * RUN // 16 : hi * RUN // 16]),
+                row[:].rearrange("q h p c -> q (h p c)"),
+                ADD,
+            )
+        s4 = s[:].rearrange("q (g r) -> q g r", r=R)
+        pair_a = sb.tile([P, HG, 2], F32, name="pair_a")
+        nc.vector.tensor_tensor(pair_a[:], s4[:, 0:HG, 0:2], s4[:, 0:HG, 2:4], MAX)
+
+        obs_codes = sb.tile([P, Q], U32, name="obs_codes", align_bytes=64)
+        obs_scales = sb.tile([P, Q], U8, name="obs_scales", align_bytes=64)
+        nc.vector.quantize_mx(
+            out=obs_codes[:].bitcast(FP8X4), scales=obs_scales[:], in_=obs_bf[:].rearrange("p q j -> p (q j)")
+        )
+        got_words = sb.tile([P, G], U32, name="got_words", align_bytes=64)
+        got_scales = sb.tile([P, G], U8, name="got_scales", align_bytes=64)
+        nc.vector.tensor_copy(got_words[:], words[:].bitcast(U32).indirect(offs_sb[:]))
+        nc.vector.tensor_copy(got_scales[:], scales[:].indirect(offs_sb[:]))
+
+        emis = ps.tile([P, G], F32, name="emis")
+        nc.tensor.matmul_mx(
+            out=emis[:],
+            lhsT=obs_codes[:].bitcast(FP8X4),
+            lhsT_scale=obs_scales[:],
+            rhs=got_words[:].bitcast(FP8X4),
+            rhs_scale=got_scales[:],
+            start=True,
+            stop=True,
+        )
+
+        pair_b = sb.tile([P, HG, 2], F32, name="pair_b", tag="words")
+        nc.vector.tensor_tensor(pair_b[:], s4[:, HG:G, 0:2], s4[:, HG:G, 2:4], MAX)
+        best_a = sb.tile([P, HG], F32, name="best_a")
+        best_b = sb.tile([P, HG], F32, name="best_b")
+        nc.vector.tensor_tensor(best_a[:], pair_a[:, :, 0], pair_a[:, :, 1], MAX)
+        nc.vector.tensor_tensor(best_b[:], pair_b[:, :, 0], pair_b[:, :, 1], MAX)
+        res_a = sb.tile([P, HG], F32, name="res_a")
+        res_b = sb.tile([P, HG], F32, name="res_b")
+        nc.vector.tensor_tensor(res_a[:], emis[:, 0:HG], best_a[:], ADD)
+        nc.scalar.dma_start(out=out[:, 0:HG], in_=res_a[:])
+        nc.vector.tensor_tensor(res_b[:], emis[:, HG:G], best_b[:], ADD)
+        nc.sync.dma_start(out=out[:, HG:G], in_=res_b[:])

@@ -17,10 +17,15 @@ ADD = mybir.AluOpType.add
 MAX = mybir.AluOpType.max
 
 P = 128
-R = 4
+PACK = 4
+QUADRANT = 32
+LIST_ROWS = 16
+R = I // G
 RUN = 256
-PIECES = ((0, 1), (1, 2), (2, 4))
+PER_RUN = RUN // P
+BLOCK_WORDS = 8
 HG = G // 2
+SPANS = ((0, 1), (1, 2), (2, 4))
 
 
 def tile_attend_viterbistep_kernel(tc, obs, emit_words, emit_scales, cum, step, offs, offs2, out):
@@ -29,69 +34,73 @@ def tile_attend_viterbistep_kernel(tc, obs, emit_words, emit_scales, cum, step, 
         sb = ctx.enter_context(tc.tile_pool(name="sb", bufs=1))
         ps = ctx.enter_context(tc.psum_pool(name="ps", bufs=1))
 
-        cum_sb = sb.tile([P, U], F32, name="cum_sb")
-        offs2_sb = sb.tile([P, I // 16], U16, name="offs2_sb")
-        offs_sb = sb.tile([P, G // 16], U16, name="offs_sb")
-        obs_sb = sb.tile([P, 4, Q], F32, name="obs_sb")
+        cum_sb = sb.tile([P, U], F32, name="cum_sb", tag="cum", align_bytes=64)
+        offs2_sb = sb.tile([P, I // LIST_ROWS], U16, name="offs2_sb")
+        offs_sb = sb.tile([P, G // LIST_ROWS], U16, name="offs_sb")
+        obs_sb = sb.tile([P, PACK, Q], F32, name="obs_sb")
         words = sb.tile([P, T], I32, name="words", tag="words")
         scales = sb.tile([P, T], U8, name="scales", tag="scales")
-        step_a = sb.tile([P, 1, 8], F32, name="step_a")
-        step_b = sb.tile([P, 3, 8], F32, name="step_b")
+        step_lo = sb.tile([P, 2, BLOCK_WORDS], F32, name="step_lo")
+        step_hi = sb.tile([P, 2 * PER_RUN], F32, name="step_hi")
+        step_cols = [step_lo[:, 0, 0:PER_RUN], step_lo[:, 1, 0:PER_RUN], step_hi[:]]
         ident = sb.tile([P, P], F32, name="ident")
 
         nc.vector.memset(scales[:].bitcast(I32), 0)
-        nc.scalar.dma_start(out=step_a[:, :, 0:2], in_=step[0, 0:RUN].rearrange("(h p c) -> p h c", h=1, c=2))
-        nc.scalar.dma_start(out=step_b[:, :, 0:2], in_=step[0, RUN:I].rearrange("(h p c) -> p h c", h=3, c=2))
-        nc.sync.dma_start(out=cum_sb[:], in_=cum)
+
+        nc.scalar.dma_start(
+            out=step_lo[:, :, 0:PER_RUN], in_=step[0, 0 : 2 * RUN].rearrange("(h p c) -> p h c", h=2, c=PER_RUN)
+        )
         nc.sync.dma_start(offs2_sb[:], offs2)
-        nc.sync.dma_start(out=obs_sb[:], in_=obs.rearrange("(p j) q -> p j q", j=4))
+        nc.sync.dma_start(out=cum_sb[:], in_=cum)
+        nc.scalar.dma_start(out=step_hi[:], in_=step[0, 2 * RUN : I].rearrange("(p c) -> p c", c=2 * PER_RUN))
+        nc.sync.dma_start(out=obs_sb[:], in_=obs.rearrange("(p j) q -> p j q", j=PACK))
         nc.sync.dma_start(out=words[:], in_=emit_words[0].rearrange("p n t -> p (n t)").bitcast(I32))
         nc.sync.dma_start(offs_sb[:], offs)
-        for quad in range(4):
+        for j in range(PACK):
             nc.sync.dma_start(
-                out=scales[32 * quad : 32 * quad + 4, :].bitcast(I32),
-                in_=emit_scales[0, 4 * quad : 4 * quad + 4, :].bitcast(I32),
+                out=scales[j:P:QUADRANT, :].bitcast(I32), in_=emit_scales[0, j : D // QUADRANT : PACK, :].bitcast(I32)
             )
         make_identity(nc, ident[:])
 
-        step_cols = [step_a[:, 0, :], step_b[:, 0, :], step_b[:, 1, :], step_b[:, 2, :]]
-        s = sb.tile([P, I], F32, name="s")
         rows = []
-        for lo, hi in PIECES:
+        for (lo, hi), cols in zip(SPANS, step_cols):
             n = hi - lo
-            spread = ps.tile([P, n, 2, P], F32, name="spread%d" % lo)
-            for h in range(n):
-                for c in range(2):
-                    nc.tensor.transpose(spread[:, h, c, :], step_cols[lo + h][:, c : c + 1].to_broadcast([P, P]), ident[:])
-            row = sb.tile([P, n, P, 2], F32, name="step_row%d" % lo)
-            nc.scalar.copy(row[:], spread[:].rearrange("q h c p -> q h p c"))
-            rows.append(row)
+            spread = ps.tile([P, PER_RUN * n, P], F32, name="spread%d" % lo)
+            for c in range(PER_RUN * n):
+                nc.tensor.transpose(spread[:, c, :], cols[:, c : c + 1].to_broadcast([P, P]), ident[:])
+            for k in range(lo, hi):
+                row = sb.tile([P, P // n, PER_RUN * n], F32, name="row%d" % k, tag="row%d" % k, align_bytes=64)
+                first = (k - lo) * P // n
+                nc.scalar.copy(row[:], spread[:, :, first : first + P // n].rearrange("q c p -> q p c"))
+                rows.append(row)
 
-        obs_bf = sb.tile([P, Q, 4], BF16, name="obs_bf", align_bytes=64)
+        s = sb.tile([P, I], F32, name="s")
+        for k, row in enumerate(rows):
+            nc.vector.tensor_tensor(
+                s[:, k * RUN : (k + 1) * RUN],
+                cum_sb[:].indirect(offs2_sb[:, k * RUN // LIST_ROWS : (k + 1) * RUN // LIST_ROWS]),
+                row[:].rearrange("q p c -> q (p c)"),
+                ADD,
+            )
+        s4 = s[:].rearrange("q (g r) -> q g r", r=R)
+
+        pair_a = sb.tile([P, HG, 2], F32, name="pair_a", tag="row2", align_bytes=64)
+        nc.vector.tensor_tensor(pair_a[:], s4[:, 0:HG, 0:2], s4[:, 0:HG, 2:4], MAX)
+
+        obs_bf = sb.tile([P, Q, PACK], BF16, name="obs_bf", tag="row0", align_bytes=64)
         nc.scalar.copy(
             obs_bf[:].rearrange("p (c i) j -> p c j i", i=4),
             obs_sb[:].rearrange("p j (c i) -> p c j i", i=4),
         )
 
-        for (lo, hi), row in zip(PIECES, rows):
-            nc.vector.tensor_tensor(
-                s[:, lo * RUN : hi * RUN],
-                cum_sb[:].indirect(offs2_sb[:, lo * RUN // 16 : hi * RUN // 16]),
-                row[:].rearrange("q h p c -> q (h p c)"),
-                ADD,
-            )
-        s4 = s[:].rearrange("q (g r) -> q g r", r=R)
-        pair_a = sb.tile([P, HG, 2], F32, name="pair_a")
-        nc.vector.tensor_tensor(pair_a[:], s4[:, 0:HG, 0:2], s4[:, 0:HG, 2:4], MAX)
-
+        got_words = sb.tile([P, G], U32, name="got_words", tag="row3", align_bytes=64)
+        got_scales = sb.tile([P, G], U8, name="got_scales", tag="cum", align_bytes=64)
         obs_codes = sb.tile([P, Q], U32, name="obs_codes", align_bytes=64)
         obs_scales = sb.tile([P, Q], U8, name="obs_scales", align_bytes=64)
+        nc.vector.tensor_copy(got_words[:], words[:].bitcast(U32).indirect(offs_sb[:]))
         nc.vector.quantize_mx(
             out=obs_codes[:].bitcast(FP8X4), scales=obs_scales[:], in_=obs_bf[:].rearrange("p q j -> p (q j)")
         )
-        got_words = sb.tile([P, G], U32, name="got_words", align_bytes=64)
-        got_scales = sb.tile([P, G], U8, name="got_scales", align_bytes=64)
-        nc.vector.tensor_copy(got_words[:], words[:].bitcast(U32).indirect(offs_sb[:]))
         nc.vector.tensor_copy(got_scales[:], scales[:].indirect(offs_sb[:]))
 
         emis = ps.tile([P, G], F32, name="emis")
@@ -107,10 +116,11 @@ def tile_attend_viterbistep_kernel(tc, obs, emit_words, emit_scales, cum, step, 
 
         pair_b = sb.tile([P, HG, 2], F32, name="pair_b", tag="words")
         nc.vector.tensor_tensor(pair_b[:], s4[:, HG:G, 0:2], s4[:, HG:G, 2:4], MAX)
-        best_a = sb.tile([P, HG], F32, name="best_a")
+        best_a = sb.tile([P, HG], F32, name="best_a", tag="scales")
         best_b = sb.tile([P, HG], F32, name="best_b")
         nc.vector.tensor_tensor(best_a[:], pair_a[:, :, 0], pair_a[:, :, 1], MAX)
         nc.vector.tensor_tensor(best_b[:], pair_b[:, :, 0], pair_b[:, :, 1], MAX)
+
         res_a = sb.tile([P, HG], F32, name="res_a")
         res_b = sb.tile([P, HG], F32, name="res_b")
         nc.vector.tensor_tensor(res_a[:], emis[:, 0:HG], best_a[:], ADD)

@@ -15,17 +15,19 @@ U8 = mybir.dt.uint8
 FP8X4 = mybir.dt.float8_e4m3fn_x4
 ADD = mybir.AluOpType.add
 MAX = mybir.AluOpType.max
+IDENT = mybir.ActivationFunctionType.Identity
 
 P = 128
 PACK = 4
 QUADRANT = 32
 LIST_ROWS = 16
 R = I // G
-RUN = 256
-PER_RUN = RUN // P
+H = G // P
+RUN = P * R
 BLOCK_WORDS = 8
+
 HG = G // 2
-SPANS = ((0, 1), (1, 2), (2, 4))
+BLOCKS = I // P
 
 
 def tile_attend_viterbistep_kernel(tc, obs, emit_words, emit_scales, cum, step, offs, offs2, out):
@@ -37,70 +39,91 @@ def tile_attend_viterbistep_kernel(tc, obs, emit_words, emit_scales, cum, step, 
         cum_sb = sb.tile([P, U], F32, name="cum_sb", tag="cum", align_bytes=64)
         offs2_sb = sb.tile([P, I // LIST_ROWS], U16, name="offs2_sb")
         offs_sb = sb.tile([P, G // LIST_ROWS], U16, name="offs_sb")
-        obs_sb = sb.tile([P, PACK, Q], F32, name="obs_sb")
+        obs_sb = sb.tile([P, PACK, Q], F32, name="obs_sb", tag="obs")
         words = sb.tile([P, T], I32, name="words", tag="words")
         scales = sb.tile([P, T], U8, name="scales", tag="scales")
-        step_lo = sb.tile([P, 2, BLOCK_WORDS], F32, name="step_lo")
-        step_hi = sb.tile([P, 2 * PER_RUN], F32, name="step_hi")
-        step_cols = [step_lo[:, 0, 0:PER_RUN], step_lo[:, 1, 0:PER_RUN], step_hi[:]]
+        step_rows = sb.tile([P, P], F32, name="step_rows")
         ident = sb.tile([P, P], F32, name="ident")
 
+        nc.vector.memset(step_rows[0 : P - BLOCKS, :], 0.0)
         nc.vector.memset(scales[:].bitcast(I32), 0)
 
-        nc.scalar.dma_start(
-            out=step_lo[:, :, 0:PER_RUN], in_=step[0, 0 : 2 * RUN].rearrange("(h p c) -> p h c", h=2, c=PER_RUN)
-        )
+        def load_scales(queue, j):
+            queue.dma_start(
+                out=scales[j:P:QUADRANT, :].bitcast(I32), in_=emit_scales[0, j : D // QUADRANT : PACK, :].bitcast(I32)
+            )
+
         nc.sync.dma_start(offs2_sb[:], offs2)
+        nc.scalar.dma_start(out=step_rows[P - BLOCKS : P, :], in_=step[0].rearrange("(k j) -> k j", j=P))
         nc.sync.dma_start(out=cum_sb[:], in_=cum)
-        nc.scalar.dma_start(out=step_hi[:], in_=step[0, 2 * RUN : I].rearrange("(p c) -> p c", c=2 * PER_RUN))
         nc.sync.dma_start(out=obs_sb[:], in_=obs.rearrange("(p j) q -> p j q", j=PACK))
         nc.sync.dma_start(out=words[:], in_=emit_words[0].rearrange("p n t -> p (n t)").bitcast(I32))
         nc.sync.dma_start(offs_sb[:], offs)
-        for j in range(PACK):
-            nc.sync.dma_start(
-                out=scales[j:P:QUADRANT, :].bitcast(I32), in_=emit_scales[0, j : D // QUADRANT : PACK, :].bitcast(I32)
-            )
+        load_scales(nc.sync, 0)
+        load_scales(nc.sync, 1)
+        load_scales(nc.sync, 2)
+        load_scales(nc.sync, 3)
+
         make_identity(nc, ident[:])
 
-        rows = []
-        for (lo, hi), cols in zip(SPANS, step_cols):
-            n = hi - lo
-            spread = ps.tile([P, PER_RUN * n, P], F32, name="spread%d" % lo)
-            for c in range(PER_RUN * n):
-                nc.tensor.transpose(spread[:, c, :], cols[:, c : c + 1].to_broadcast([P, P]), ident[:])
-            for k in range(lo, hi):
-                row = sb.tile([P, P // n, PER_RUN * n], F32, name="row%d" % k, tag="row%d" % k, align_bytes=64)
-                first = (k - lo) * P // n
-                nc.scalar.copy(row[:], spread[:, :, first : first + P // n].rearrange("q c p -> q p c"))
-                rows.append(row)
+        turned = ps.tile([P, P], F32, name="turned")
+        nc.tensor.transpose(turned[:], step_rows[:], ident[:])
+        cols_b = sb.tile([P, R], F32, name="cols_b", tag="cols_b", align_bytes=64)
+        nc.scalar.copy(cols_b[:], turned[:, P - R : P])
+        step_cols = sb.tile([P, R], F32, name="step_cols")
+        nc.scalar.copy(step_cols[:], turned[:, P - BLOCKS : P - R])
 
-        s = sb.tile([P, I], F32, name="s")
-        for k, row in enumerate(rows):
+        rows = []
+        for k in range(2):
+            spread = ps.tile([P, 2, P], F32, name="spread%d" % k, tag="spread%d" % k)
+            for c in range(2):
+                col = 2 * k + c
+                nc.tensor.transpose(spread[:, c, :], cols_b[:, col : col + 1].to_broadcast([P, P]), ident[:])
+            row = sb.tile([P, 2 * P], F32, name="row%d" % k, tag="row%d" % k, align_bytes=64)
+            nc.scalar.copy(row[:], spread[:].rearrange("q c p -> q (c p)"))
+            rows.append(row)
+
+        got_a = sb.tile([P, RUN], F32, name="got_a")
+        s_b = sb.tile([P, RUN], F32, name="s_b")
+        nc.vector.tensor_copy(got_a[:], cum_sb[:].indirect(offs2_sb[:, 0 : RUN // LIST_ROWS]))
+        for k in range(2):
+            lo = RUN + 2 * P * k
             nc.vector.tensor_tensor(
-                s[:, k * RUN : (k + 1) * RUN],
-                cum_sb[:].indirect(offs2_sb[:, k * RUN // LIST_ROWS : (k + 1) * RUN // LIST_ROWS]),
-                row[:].rearrange("q p c -> q (p c)"),
+                s_b[:, 2 * P * k : 2 * P * (k + 1)],
+                cum_sb[:].indirect(offs2_sb[:, lo // LIST_ROWS : (lo + 2 * P) // LIST_ROWS]),
+                rows[k][:],
                 ADD,
             )
-        s4 = s[:].rearrange("q (g r) -> q g r", r=R)
+        s4 = s_b[:].rearrange("q (g r) -> q g r", r=R)
 
-        pair_a = sb.tile([P, HG, 2], F32, name="pair_a", tag="row2", align_bytes=64)
-        nc.vector.tensor_tensor(pair_a[:], s4[:, 0:HG, 0:2], s4[:, 0:HG, 2:4], MAX)
-
-        obs_bf = sb.tile([P, Q, PACK], BF16, name="obs_bf", tag="row0", align_bytes=64)
+        obs_bf = sb.tile([P, Q, PACK], BF16, name="obs_bf", tag="cols_b", align_bytes=64)
         nc.scalar.copy(
             obs_bf[:].rearrange("p (c i) j -> p c j i", i=4),
             obs_sb[:].rearrange("p j (c i) -> p c j i", i=4),
         )
 
-        got_words = sb.tile([P, G], U32, name="got_words", tag="row3", align_bytes=64)
+        down = ps.tile([P, R, P], F32, name="down", tag="spread1")
+        for k in range(R):
+            nc.tensor.transpose(down[:, k, :], got_a[:, k * P : (k + 1) * P], ident[:])
+        sums = sb.tile([P, R, P], F32, name="sums", tag="obs")
+        s_a = ps.tile([P, R, P], F32, name="s_a")
+        for k in range(R):
+            nc.scalar.activation(sums[:, k, :], down[:, k, :], IDENT, bias=step_cols[:, k : k + 1])
+            nc.tensor.transpose(s_a[:, k, :], sums[:, k, :], ident[:])
+
+        got_words = sb.tile([P, G], U32, name="got_words", tag="row1", align_bytes=64)
         got_scales = sb.tile([P, G], U8, name="got_scales", tag="cum", align_bytes=64)
         obs_codes = sb.tile([P, Q], U32, name="obs_codes", align_bytes=64)
         obs_scales = sb.tile([P, Q], U8, name="obs_scales", align_bytes=64)
-        nc.vector.tensor_copy(got_words[:], words[:].bitcast(U32).indirect(offs_sb[:]))
+
+        pair_b = sb.tile([P, HG, 2], F32, name="pair_b")
+        best_b = sb.tile([P, HG], F32, name="best_b")
         nc.vector.quantize_mx(
             out=obs_codes[:].bitcast(FP8X4), scales=obs_scales[:], in_=obs_bf[:].rearrange("p q j -> p (q j)")
         )
+        nc.vector.tensor_tensor(pair_b[:], s4[:, :, 0:2], s4[:, :, 2:4], MAX)
+        nc.vector.tensor_copy(got_words[:], words[:].bitcast(U32).indirect(offs_sb[:]))
+        nc.vector.tensor_tensor(best_b[:], pair_b[:, :, 0], pair_b[:, :, 1], MAX)
         nc.vector.tensor_copy(got_scales[:], scales[:].indirect(offs_sb[:]))
 
         emis = ps.tile([P, G], F32, name="emis")
@@ -114,16 +137,14 @@ def tile_attend_viterbistep_kernel(tc, obs, emit_words, emit_scales, cum, step, 
             stop=True,
         )
 
-        pair_b = sb.tile([P, HG, 2], F32, name="pair_b", tag="words")
-        nc.vector.tensor_tensor(pair_b[:], s4[:, HG:G, 0:2], s4[:, HG:G, 2:4], MAX)
         best_a = sb.tile([P, HG], F32, name="best_a", tag="scales")
-        best_b = sb.tile([P, HG], F32, name="best_b")
-        nc.vector.tensor_tensor(best_a[:], pair_a[:, :, 0], pair_a[:, :, 1], MAX)
-        nc.vector.tensor_tensor(best_b[:], pair_b[:, :, 0], pair_b[:, :, 1], MAX)
+        nc.vector.tensor_reduce(
+            best_a[:], s_a[:].rearrange("q k (g r) -> q (k g) r", r=R), mybir.AxisListType.X, MAX
+        )
 
         res_a = sb.tile([P, HG], F32, name="res_a")
         res_b = sb.tile([P, HG], F32, name="res_b")
-        nc.vector.tensor_tensor(res_a[:], emis[:, 0:HG], best_a[:], ADD)
-        nc.scalar.dma_start(out=out[:, 0:HG], in_=res_a[:])
         nc.vector.tensor_tensor(res_b[:], emis[:, HG:G], best_b[:], ADD)
-        nc.sync.dma_start(out=out[:, HG:G], in_=res_b[:])
+        nc.scalar.dma_start(out=out[:, HG:G], in_=res_b[:])
+        nc.vector.tensor_tensor(res_a[:], emis[:, 0:HG], best_a[:], ADD)
+        nc.sync.dma_start(out=out[:, 0:HG], in_=res_a[:])

@@ -35,11 +35,12 @@ def tile_attend_viterbistep_kernel(tc, obs, emit_words, emit_scales, cum, step, 
     with ExitStack() as ctx:
         sb = ctx.enter_context(tc.tile_pool(name="sb", bufs=1))
         ps = ctx.enter_context(tc.psum_pool(name="ps", bufs=1))
+        shared = ctx.enter_context(tc.tile_pool(name="shared", bufs=1))
 
         cum_sb = sb.tile([P, U], F32, name="cum_sb", tag="cum", align_bytes=64)
         offs2_sb = sb.tile([P, I // LIST_ROWS], U16, name="offs2_sb")
         offs_sb = sb.tile([P, G // LIST_ROWS], U16, name="offs_sb")
-        obs_sb = sb.tile([P, PACK, Q], F32, name="obs_sb", tag="obs")
+        obs_sb = shared.tile([P, PACK, Q], F32, name="obs_sb", offset=0)
         words = sb.tile([P, T], I32, name="words", tag="words")
         scales = sb.tile([P, T], U8, name="scales", tag="scales")
         step_rows = sb.tile([P, P], F32, name="step_rows")
@@ -53,12 +54,12 @@ def tile_attend_viterbistep_kernel(tc, obs, emit_words, emit_scales, cum, step, 
                 out=scales[j:P:QUADRANT, :].bitcast(I32), in_=emit_scales[0, j : D // QUADRANT : PACK, :].bitcast(I32)
             )
 
+        nc.sync.dma_start(out=step_rows[P - BLOCKS : P, :], in_=step[0].rearrange("(k j) -> k j", j=P))
+        nc.scalar.dma_start(out=cum_sb[:], in_=cum)
         nc.sync.dma_start(offs2_sb[:], offs2)
-        nc.scalar.dma_start(out=step_rows[P - BLOCKS : P, :], in_=step[0].rearrange("(k j) -> k j", j=P))
-        nc.sync.dma_start(out=cum_sb[:], in_=cum)
-        nc.sync.dma_start(out=obs_sb[:], in_=obs.rearrange("(p j) q -> p j q", j=PACK))
-        nc.sync.dma_start(out=words[:], in_=emit_words[0].rearrange("p n t -> p (n t)").bitcast(I32))
+        nc.scalar.dma_start(out=obs_sb[:], in_=obs.rearrange("(p j) q -> p j q", j=PACK))
         nc.sync.dma_start(offs_sb[:], offs)
+        nc.scalar.dma_start(out=words[:], in_=emit_words[0].rearrange("p n t -> p (n t)").bitcast(I32))
         load_scales(nc.sync, 0)
         load_scales(nc.sync, 1)
         load_scales(nc.sync, 2)
@@ -105,7 +106,7 @@ def tile_attend_viterbistep_kernel(tc, obs, emit_words, emit_scales, cum, step, 
         down = ps.tile([P, R, P], F32, name="down", tag="spread1")
         for k in range(R):
             nc.tensor.transpose(down[:, k, :], got_a[:, k * P : (k + 1) * P], ident[:])
-        sums = sb.tile([P, R, P], F32, name="sums", tag="obs")
+        sums = shared.tile([P, R, P], F32, name="sums", offset=0)
         s_a = ps.tile([P, R, P], F32, name="s_a")
         for k in range(R):
             nc.scalar.activation(sums[:, k, :], down[:, k, :], IDENT, bias=step_cols[:, k : k + 1])
@@ -117,13 +118,11 @@ def tile_attend_viterbistep_kernel(tc, obs, emit_words, emit_scales, cum, step, 
         obs_scales = sb.tile([P, Q], U8, name="obs_scales", align_bytes=64)
 
         pair_b = sb.tile([P, HG, 2], F32, name="pair_b")
-        best_b = sb.tile([P, HG], F32, name="best_b")
         nc.vector.quantize_mx(
             out=obs_codes[:].bitcast(FP8X4), scales=obs_scales[:], in_=obs_bf[:].rearrange("p q j -> p (q j)")
         )
         nc.vector.tensor_tensor(pair_b[:], s4[:, :, 0:2], s4[:, :, 2:4], MAX)
         nc.vector.tensor_copy(got_words[:], words[:].bitcast(U32).indirect(offs_sb[:]))
-        nc.vector.tensor_tensor(best_b[:], pair_b[:, :, 0], pair_b[:, :, 1], MAX)
         nc.vector.tensor_copy(got_scales[:], scales[:].indirect(offs_sb[:]))
 
         emis = ps.tile([P, G], F32, name="emis")
@@ -137,14 +136,16 @@ def tile_attend_viterbistep_kernel(tc, obs, emit_words, emit_scales, cum, step, 
             stop=True,
         )
 
-        best_a = sb.tile([P, HG], F32, name="best_a", tag="scales")
+        best_a = sb.tile([P, HG], F32, name="best_a")
         nc.vector.tensor_reduce(
             best_a[:], s_a[:].rearrange("q k (g r) -> q (k g) r", r=R), mybir.AxisListType.X, MAX
         )
 
+        best_b = shared.tile([P, HG], F32, name="best_b", offset=0)
+        nc.vector.tensor_tensor(best_b[:], pair_b[:, :, 0], pair_b[:, :, 1], MAX)
         res_a = sb.tile([P, HG], F32, name="res_a")
         res_b = sb.tile([P, HG], F32, name="res_b")
-        nc.vector.tensor_tensor(res_b[:], emis[:, HG:G], best_b[:], ADD)
-        nc.scalar.dma_start(out=out[:, HG:G], in_=res_b[:])
         nc.vector.tensor_tensor(res_a[:], emis[:, 0:HG], best_a[:], ADD)
-        nc.sync.dma_start(out=out[:, 0:HG], in_=res_a[:])
+        nc.scalar.dma_start(out=out[:, 0:HG], in_=res_a[:])
+        nc.vector.tensor_tensor(res_b[:], emis[:, HG:G], best_b[:], ADD)
+        nc.sync.dma_start(out=out[:, HG:G], in_=res_b[:])

@@ -28,6 +28,7 @@ BLOCK_WORDS = 8
 
 HG = G // 2
 BLOCKS = I // P
+RUN4 = 2 * P
 
 
 def tile_attend_viterbistep_kernel(tc, obs, emit_words, emit_scales, cum, step, offs, offs2, out):
@@ -46,84 +47,83 @@ def tile_attend_viterbistep_kernel(tc, obs, emit_words, emit_scales, cum, step, 
         step_rows = sb.tile([P, P], F32, name="step_rows")
         ident = sb.tile([P, P], F32, name="ident")
 
+        nc.gpsimd.memset(scales[:].bitcast(I32), 0)
         nc.vector.memset(step_rows[0 : P - BLOCKS, :], 0.0)
-        nc.vector.memset(scales[:].bitcast(I32), 0)
 
         def load_scales(queue, j):
             queue.dma_start(
                 out=scales[j:P:QUADRANT, :].bitcast(I32), in_=emit_scales[0, j : D // QUADRANT : PACK, :].bitcast(I32)
             )
 
-        nc.sync.dma_start(out=step_rows[P - BLOCKS : P, :], in_=step[0].rearrange("(k j) -> k j", j=P))
-        nc.scalar.dma_start(out=cum_sb[:], in_=cum)
         nc.sync.dma_start(offs2_sb[:], offs2)
-        nc.scalar.dma_start(out=obs_sb[:], in_=obs.rearrange("(p j) q -> p j q", j=PACK))
+        nc.scalar.dma_start(out=step_rows[P - BLOCKS : P, :], in_=step[0].rearrange("(k j) -> k j", j=P))
+        nc.sync.dma_start(out=cum_sb[:], in_=cum)
+        nc.sync.dma_start(out=obs_sb[:], in_=obs.rearrange("(p j) q -> p j q", j=PACK))
         nc.sync.dma_start(offs_sb[:], offs)
-        nc.scalar.dma_start(out=words[:], in_=emit_words[0].rearrange("p n t -> p (n t)").bitcast(I32))
         load_scales(nc.sync, 0)
         load_scales(nc.sync, 1)
         load_scales(nc.sync, 2)
         load_scales(nc.sync, 3)
+        nc.sync.dma_start(out=words[:], in_=emit_words[0].rearrange("p n t -> p (n t)").bitcast(I32))
 
         make_identity(nc, ident[:])
 
         turned = ps.tile([P, P], F32, name="turned")
         nc.tensor.transpose(turned[:], step_rows[:], ident[:])
-        cols_b = sb.tile([P, R], F32, name="cols_b", tag="cols_b", align_bytes=64)
-        nc.scalar.copy(cols_b[:], turned[:, P - R : P])
-        step_cols = sb.tile([P, R], F32, name="step_cols")
-        nc.scalar.copy(step_cols[:], turned[:, P - BLOCKS : P - R])
+        cols = sb.tile([P, BLOCKS], F32, name="cols", tag="cols", align_bytes=64)
+        nc.scalar.copy(cols[:], turned[:, P - BLOCKS : P])
 
         rows = []
-        for k in range(2):
+        for k in range(1, R):
             spread = ps.tile([P, 2, P], F32, name="spread%d" % k, tag="spread%d" % k)
             for c in range(2):
-                col = 2 * k + c
-                nc.tensor.transpose(spread[:, c, :], cols_b[:, col : col + 1].to_broadcast([P, P]), ident[:])
-            row = sb.tile([P, 2 * P], F32, name="row%d" % k, tag="row%d" % k, align_bytes=64)
+                nc.tensor.transpose(spread[:, c, :], cols[:, 2 * k + c : 2 * k + c + 1].to_broadcast([P, P]), ident[:])
+            row = sb.tile([P, RUN4], F32, name="row%d" % k, tag="row%d" % k, align_bytes=64)
             nc.scalar.copy(row[:], spread[:].rearrange("q c p -> q (c p)"))
             rows.append(row)
 
-        got_a = sb.tile([P, RUN], F32, name="got_a")
-        s_b = sb.tile([P, RUN], F32, name="s_b")
-        nc.vector.tensor_copy(got_a[:], cum_sb[:].indirect(offs2_sb[:, 0 : RUN // LIST_ROWS]))
-        for k in range(2):
-            lo = RUN + 2 * P * k
+        first = sb.tile([P, RUN4], F32, name="first")
+        s = sb.tile([P, I], F32, name="s")
+        nc.vector.tensor_copy(first[:], cum_sb[:].indirect(offs2_sb[:, 0 : RUN4 // LIST_ROWS]))
+        for k in range(1, R):
             nc.vector.tensor_tensor(
-                s_b[:, 2 * P * k : 2 * P * (k + 1)],
-                cum_sb[:].indirect(offs2_sb[:, lo // LIST_ROWS : (lo + 2 * P) // LIST_ROWS]),
-                rows[k][:],
+                s[:, k * RUN4 : (k + 1) * RUN4],
+                cum_sb[:].indirect(offs2_sb[:, k * RUN4 // LIST_ROWS : (k + 1) * RUN4 // LIST_ROWS]),
+                rows[k - 1][:],
                 ADD,
             )
-        s4 = s_b[:].rearrange("q (g r) -> q g r", r=R)
 
-        obs_bf = sb.tile([P, Q, PACK], BF16, name="obs_bf", tag="cols_b", align_bytes=64)
+        down = ps.tile([P, 2, P], F32, name="down", tag="spread1")
+        for c in range(2):
+            nc.tensor.transpose(down[:, c, :], first[:, c * P : (c + 1) * P], ident[:])
+        sums = sb.tile([P, 2, P], F32, name="sums", tag="sums", align_bytes=64)
+        up = ps.tile([P, 2, P], F32, name="up")
+        for c in range(2):
+            nc.scalar.activation(sums[:, c, :], down[:, c, :], IDENT, bias=cols[:, c : c + 1])
+            nc.tensor.transpose(up[:, c, :], sums[:, c, :], ident[:])
+        nc.scalar.copy(s[:, 0:RUN4], up[:].rearrange("q c p -> q (c p)"))
+        s4 = s[:].rearrange("q (g r) -> q g r", r=R)
+
+        obs_bf = sb.tile([P, Q, PACK], BF16, name="obs_bf", tag="cols", align_bytes=64)
         nc.scalar.copy(
             obs_bf[:].rearrange("p (c i) j -> p c j i", i=4),
             obs_sb[:].rearrange("p j (c i) -> p c j i", i=4),
         )
 
-        down = ps.tile([P, R, P], F32, name="down", tag="spread1")
-        for k in range(R):
-            nc.tensor.transpose(down[:, k, :], got_a[:, k * P : (k + 1) * P], ident[:])
-        sums = shared.tile([P, R, P], F32, name="sums", offset=0)
-        s_a = ps.tile([P, R, P], F32, name="s_a")
-        for k in range(R):
-            nc.scalar.activation(sums[:, k, :], down[:, k, :], IDENT, bias=step_cols[:, k : k + 1])
-            nc.tensor.transpose(s_a[:, k, :], sums[:, k, :], ident[:])
-
-        got_words = sb.tile([P, G], U32, name="got_words", tag="row1", align_bytes=64)
-        got_scales = sb.tile([P, G], U8, name="got_scales", tag="cum", align_bytes=64)
+        got_words = sb.tile([P, G], U32, name="got_words", tag="row3", align_bytes=64)
+        got_scales = sb.tile([P, G], U8, name="got_scales", tag="row2", align_bytes=64)
         obs_codes = sb.tile([P, Q], U32, name="obs_codes", align_bytes=64)
         obs_scales = sb.tile([P, Q], U8, name="obs_scales", align_bytes=64)
+        nc.vector.tensor_copy(got_scales[:], scales[:].indirect(offs_sb[:]))
+        nc.vector.tensor_copy(got_words[:], words[:].bitcast(U32).indirect(offs_sb[:]))
 
-        pair_b = sb.tile([P, HG, 2], F32, name="pair_b")
+        pair_a = sb.tile([P, HG, 2], F32, name="pair_a")
+        pair_b = shared.tile([P, HG, 2], F32, name="pair_b", offset=0)
+        best_a = sb.tile([P, HG], F32, name="best_a")
+        best_b = sb.tile([P, HG], F32, name="best_b")
         nc.vector.quantize_mx(
             out=obs_codes[:].bitcast(FP8X4), scales=obs_scales[:], in_=obs_bf[:].rearrange("p q j -> p (q j)")
         )
-        nc.vector.tensor_tensor(pair_b[:], s4[:, :, 0:2], s4[:, :, 2:4], MAX)
-        nc.vector.tensor_copy(got_words[:], words[:].bitcast(U32).indirect(offs_sb[:]))
-        nc.vector.tensor_copy(got_scales[:], scales[:].indirect(offs_sb[:]))
 
         emis = ps.tile([P, G], F32, name="emis")
         nc.tensor.matmul_mx(
@@ -136,16 +136,13 @@ def tile_attend_viterbistep_kernel(tc, obs, emit_words, emit_scales, cum, step, 
             stop=True,
         )
 
-        best_a = sb.tile([P, HG], F32, name="best_a")
-        nc.vector.tensor_reduce(
-            best_a[:], s_a[:].rearrange("q k (g r) -> q (k g) r", r=R), mybir.AxisListType.X, MAX
-        )
-
-        best_b = shared.tile([P, HG], F32, name="best_b", offset=0)
+        nc.vector.tensor_tensor(pair_b[:], s4[:, HG:G, 0:2], s4[:, HG:G, 2:4], MAX)
+        nc.vector.tensor_tensor(pair_a[:], s4[:, 0:HG, 0:2], s4[:, 0:HG, 2:4], MAX)
         nc.vector.tensor_tensor(best_b[:], pair_b[:, :, 0], pair_b[:, :, 1], MAX)
+        nc.vector.tensor_tensor(best_a[:], pair_a[:, :, 0], pair_a[:, :, 1], MAX)
         res_a = sb.tile([P, HG], F32, name="res_a")
         res_b = sb.tile([P, HG], F32, name="res_b")
-        nc.vector.tensor_tensor(res_a[:], emis[:, 0:HG], best_a[:], ADD)
-        nc.scalar.dma_start(out=out[:, 0:HG], in_=res_a[:])
         nc.vector.tensor_tensor(res_b[:], emis[:, HG:G], best_b[:], ADD)
-        nc.sync.dma_start(out=out[:, HG:G], in_=res_b[:])
+        nc.scalar.dma_start(out=out[:, HG:G], in_=res_b[:])
+        nc.vector.tensor_tensor(res_a[:], emis[:, 0:HG], best_a[:], ADD)
+        nc.sync.dma_start(out=out[:, 0:HG], in_=res_a[:])

@@ -28,7 +28,8 @@ BLOCK_WORDS = 8
 
 HG = G // 2
 BLOCKS = I // P
-RUN4 = 2 * P
+PLAIN = 3
+FUSED = ((3, 5), (5, 8))
 
 
 def tile_attend_viterbistep_kernel(tc, obs, emit_words, emit_scales, cum, step, offs, offs2, out):
@@ -72,37 +73,28 @@ def tile_attend_viterbistep_kernel(tc, obs, emit_words, emit_scales, cum, step, 
         nc.tensor.transpose(turned[:], step_rows[:], ident[:])
         cols = sb.tile([P, BLOCKS], F32, name="cols", tag="cols", align_bytes=64)
         nc.scalar.copy(cols[:], turned[:, P - BLOCKS : P])
+        bias = sb.tile([P, PLAIN], F32, name="bias")
+        nc.scalar.copy(bias[:], turned[:, P - BLOCKS : P - BLOCKS + PLAIN])
 
         rows = []
-        for k in range(1, R):
-            spread = ps.tile([P, 2, P], F32, name="spread%d" % k, tag="spread%d" % k)
-            for c in range(2):
-                nc.tensor.transpose(spread[:, c, :], cols[:, 2 * k + c : 2 * k + c + 1].to_broadcast([P, P]), ident[:])
-            row = sb.tile([P, RUN4], F32, name="row%d" % k, tag="row%d" % k, align_bytes=64)
+        for lo, hi in FUSED:
+            spread = ps.tile([P, hi - lo, P], F32, name="spread%d" % lo, tag="spread%d" % lo)
+            for c in range(lo, hi):
+                nc.tensor.transpose(spread[:, c - lo, :], cols[:, c : c + 1].to_broadcast([P, P]), ident[:])
+            row = sb.tile([P, (hi - lo) * P], F32, name="row%d" % lo, tag="row%d" % lo, align_bytes=64)
             nc.scalar.copy(row[:], spread[:].rearrange("q c p -> q (c p)"))
             rows.append(row)
 
-        first = sb.tile([P, RUN4], F32, name="first")
+        first = sb.tile([P, PLAIN * P], F32, name="first")
         s = sb.tile([P, I], F32, name="s")
-        nc.vector.tensor_copy(first[:], cum_sb[:].indirect(offs2_sb[:, 0 : RUN4 // LIST_ROWS]))
-        for k in range(1, R):
+        nc.vector.tensor_copy(first[:], cum_sb[:].indirect(offs2_sb[:, 0 : PLAIN * P // LIST_ROWS]))
+        for (lo, hi), row in zip(FUSED, rows):
             nc.vector.tensor_tensor(
-                s[:, k * RUN4 : (k + 1) * RUN4],
-                cum_sb[:].indirect(offs2_sb[:, k * RUN4 // LIST_ROWS : (k + 1) * RUN4 // LIST_ROWS]),
-                rows[k - 1][:],
+                s[:, lo * P : hi * P],
+                cum_sb[:].indirect(offs2_sb[:, lo * P // LIST_ROWS : hi * P // LIST_ROWS]),
+                row[:],
                 ADD,
             )
-
-        down = ps.tile([P, 2, P], F32, name="down", tag="spread1")
-        for c in range(2):
-            nc.tensor.transpose(down[:, c, :], first[:, c * P : (c + 1) * P], ident[:])
-        sums = sb.tile([P, 2, P], F32, name="sums", tag="sums", align_bytes=64)
-        up = ps.tile([P, 2, P], F32, name="up")
-        for c in range(2):
-            nc.scalar.activation(sums[:, c, :], down[:, c, :], IDENT, bias=cols[:, c : c + 1])
-            nc.tensor.transpose(up[:, c, :], sums[:, c, :], ident[:])
-        nc.scalar.copy(s[:, 0:RUN4], up[:].rearrange("q c p -> q (c p)"))
-        s4 = s[:].rearrange("q (g r) -> q g r", r=R)
 
         obs_bf = sb.tile([P, Q, PACK], BF16, name="obs_bf", tag="cols", align_bytes=64)
         nc.scalar.copy(
@@ -110,8 +102,20 @@ def tile_attend_viterbistep_kernel(tc, obs, emit_words, emit_scales, cum, step, 
             obs_sb[:].rearrange("p j (c i) -> p c j i", i=4),
         )
 
-        got_words = sb.tile([P, G], U32, name="got_words", tag="row3", align_bytes=64)
-        got_scales = sb.tile([P, G], U8, name="got_scales", tag="row2", align_bytes=64)
+        down = ps.tile([P, PLAIN, P], F32, name="down", tag="spread%d" % FUSED[0][0])
+        for c in range(PLAIN):
+            nc.tensor.transpose(down[:, c, :], first[:, c * P : (c + 1) * P], ident[:])
+        sums = shared.tile([P, PLAIN, P], F32, name="sums", offset=0)
+        for lo, hi in ((0, PLAIN - 1), (PLAIN - 1, PLAIN)):
+            up = ps.tile([P, hi - lo, P], F32, name="up%d" % lo)
+            for c in range(lo, hi):
+                nc.scalar.activation(sums[:, c, :], down[:, c, :], IDENT, bias=bias[:, c : c + 1])
+                nc.tensor.transpose(up[:, c - lo, :], sums[:, c, :], ident[:])
+            nc.scalar.copy(s[:, lo * P : hi * P], up[:].rearrange("q c p -> q (c p)"))
+        s4 = s[:].rearrange("q (g r) -> q g r", r=R)
+
+        got_words = sb.tile([P, G], U32, name="got_words", tag="row%d" % FUSED[-1][0], align_bytes=64)
+        got_scales = sb.tile([P, G], U8, name="got_scales", tag="row%d" % FUSED[-2][0], align_bytes=64)
         obs_codes = sb.tile([P, Q], U32, name="obs_codes", align_bytes=64)
         obs_scales = sb.tile([P, Q], U8, name="obs_scales", align_bytes=64)
         nc.vector.tensor_copy(got_scales[:], scales[:].indirect(offs_sb[:]))
@@ -125,7 +129,7 @@ def tile_attend_viterbistep_kernel(tc, obs, emit_words, emit_scales, cum, step, 
             out=obs_codes[:].bitcast(FP8X4), scales=obs_scales[:], in_=obs_bf[:].rearrange("p q j -> p (q j)")
         )
 
-        emis = ps.tile([P, G], F32, name="emis")
+        emis = ps.tile([P, G], F32, name="emis", tag="spread%d" % FUSED[0][0])
         nc.tensor.matmul_mx(
             out=emis[:],
             lhsT=obs_codes[:].bitcast(FP8X4),

@@ -15,21 +15,18 @@ U8 = mybir.dt.uint8
 FP8X4 = mybir.dt.float8_e4m3fn_x4
 ADD = mybir.AluOpType.add
 MAX = mybir.AluOpType.max
-IDENT = mybir.ActivationFunctionType.Identity
+IDENTITY = mybir.ActivationFunctionType.Identity
 
 P = 128
 PACK = 4
 QUADRANT = 32
 LIST_ROWS = 16
 R = I // G
-H = G // P
-RUN = P * R
-BLOCK_WORDS = 8
-
 HG = G // 2
-BLOCKS = I // P
+STRIPS = I // P
 PLAIN = 3
-FUSED = ((3, 5), (5, 8))
+FUSED = ((PLAIN, PLAIN + 2), (PLAIN + 2, STRIPS))
+RETURNS = ((0, PLAIN - 1), (PLAIN - 1, PLAIN))
 
 
 def tile_attend_viterbistep_kernel(tc, obs, emit_words, emit_scales, cum, step, offs, offs2, out):
@@ -37,99 +34,95 @@ def tile_attend_viterbistep_kernel(tc, obs, emit_words, emit_scales, cum, step, 
     with ExitStack() as ctx:
         sb = ctx.enter_context(tc.tile_pool(name="sb", bufs=1))
         ps = ctx.enter_context(tc.psum_pool(name="ps", bufs=1))
-        shared = ctx.enter_context(tc.tile_pool(name="shared", bufs=1))
+
+        def entries(lo, hi):
+            return offs2_sb[:, lo * P // LIST_ROWS : hi * P // LIST_ROWS]
 
         cum_sb = sb.tile([P, U], F32, name="cum_sb", tag="cum", align_bytes=64)
         offs2_sb = sb.tile([P, I // LIST_ROWS], U16, name="offs2_sb")
         offs_sb = sb.tile([P, G // LIST_ROWS], U16, name="offs_sb")
-        obs_sb = shared.tile([P, PACK, Q], F32, name="obs_sb", offset=0)
-        words = sb.tile([P, T], I32, name="words", tag="words")
-        scales = sb.tile([P, T], U8, name="scales", tag="scales")
+        obs_sb = sb.tile([P, PACK, Q], F32, name="obs_sb", tag="obs")
+        words = sb.tile([P, T], I32, name="words")
+        scales = sb.tile([P, T], U8, name="scales")
         step_rows = sb.tile([P, P], F32, name="step_rows")
         ident = sb.tile([P, P], F32, name="ident")
 
         nc.gpsimd.memset(scales[:].bitcast(I32), 0)
-        nc.vector.memset(step_rows[0 : P - BLOCKS, :], 0.0)
-
-        def load_scales(queue, j):
-            queue.dma_start(
-                out=scales[j:P:QUADRANT, :].bitcast(I32), in_=emit_scales[0, j : D // QUADRANT : PACK, :].bitcast(I32)
-            )
+        top = P - STRIPS
+        nc.vector.memset(step_rows[0:top, :], 0.0)
 
         nc.sync.dma_start(offs2_sb[:], offs2)
-        nc.scalar.dma_start(out=step_rows[P - BLOCKS : P, :], in_=step[0].rearrange("(k j) -> k j", j=P))
+        nc.scalar.dma_start(out=step_rows[top:P, :], in_=step[0].rearrange("(k j) -> k j", j=P))
         nc.sync.dma_start(out=cum_sb[:], in_=cum)
         nc.sync.dma_start(out=obs_sb[:], in_=obs.rearrange("(p j) q -> p j q", j=PACK))
         nc.sync.dma_start(offs_sb[:], offs)
-        load_scales(nc.sync, 0)
-        load_scales(nc.sync, 1)
-        load_scales(nc.sync, 2)
-        load_scales(nc.sync, 3)
+        for j in range(PACK):
+            nc.sync.dma_start(
+                out=scales[j:P:QUADRANT, :].bitcast(I32), in_=emit_scales[0, j : D // QUADRANT : PACK, :].bitcast(I32)
+            )
         nc.sync.dma_start(out=words[:], in_=emit_words[0].rearrange("p n t -> p (n t)").bitcast(I32))
 
         make_identity(nc, ident[:])
 
         turned = ps.tile([P, P], F32, name="turned")
         nc.tensor.transpose(turned[:], step_rows[:], ident[:])
-        cols = sb.tile([P, BLOCKS], F32, name="cols", tag="cols", align_bytes=64)
-        nc.scalar.copy(cols[:], turned[:, P - BLOCKS : P])
-        bias = sb.tile([P, PLAIN], F32, name="bias")
-        nc.scalar.copy(bias[:], turned[:, P - BLOCKS : P - BLOCKS + PLAIN])
+        fused_cols = sb.tile([P, STRIPS - PLAIN], F32, name="fused_cols", tag="fused_cols", align_bytes=64)
+        nc.scalar.copy(fused_cols[:], turned[:, top + PLAIN : P])
+        plain_cols = sb.tile([P, PLAIN], F32, name="plain_cols")
+        nc.scalar.copy(plain_cols[:], turned[:, top : top + PLAIN])
 
         rows = []
         for lo, hi in FUSED:
             spread = ps.tile([P, hi - lo, P], F32, name="spread%d" % lo, tag="spread%d" % lo)
-            for c in range(lo, hi):
-                nc.tensor.transpose(spread[:, c - lo, :], cols[:, c : c + 1].to_broadcast([P, P]), ident[:])
+            for k in range(lo, hi):
+                column = fused_cols[:, k - PLAIN : k - PLAIN + 1]
+                nc.tensor.transpose(spread[:, k - lo, :], column.to_broadcast([P, P]), ident[:])
             row = sb.tile([P, (hi - lo) * P], F32, name="row%d" % lo, tag="row%d" % lo, align_bytes=64)
-            nc.scalar.copy(row[:], spread[:].rearrange("q c p -> q (c p)"))
+            nc.scalar.copy(row[:], spread[:].rearrange("q k p -> q (k p)"))
             rows.append(row)
+        first_spread_tag = "spread%d" % FUSED[0][0]
+        last_row_tag = "row%d" % FUSED[-1][0]
 
-        first = sb.tile([P, PLAIN * P], F32, name="first")
+        picked = sb.tile([P, PLAIN * P], F32, name="picked")
         s = sb.tile([P, I], F32, name="s")
-        nc.vector.tensor_copy(first[:], cum_sb[:].indirect(offs2_sb[:, 0 : PLAIN * P // LIST_ROWS]))
+        nc.vector.tensor_copy(picked[:], cum_sb[:].indirect(entries(0, PLAIN)))
         for (lo, hi), row in zip(FUSED, rows):
-            nc.vector.tensor_tensor(
-                s[:, lo * P : hi * P],
-                cum_sb[:].indirect(offs2_sb[:, lo * P // LIST_ROWS : hi * P // LIST_ROWS]),
-                row[:],
-                ADD,
-            )
+            nc.vector.tensor_tensor(s[:, lo * P : hi * P], cum_sb[:].indirect(entries(lo, hi)), row[:], ADD)
 
-        obs_bf = sb.tile([P, Q, PACK], BF16, name="obs_bf", tag="cols", align_bytes=64)
+        obs_bf = sb.tile([P, Q, PACK], BF16, name="obs_bf", tag="fused_cols", align_bytes=64)
         nc.scalar.copy(
             obs_bf[:].rearrange("p (c i) j -> p c j i", i=4),
             obs_sb[:].rearrange("p j (c i) -> p c j i", i=4),
         )
 
-        down = ps.tile([P, PLAIN, P], F32, name="down", tag="spread%d" % FUSED[0][0])
-        for c in range(PLAIN):
-            nc.tensor.transpose(down[:, c, :], first[:, c * P : (c + 1) * P], ident[:])
-        sums = shared.tile([P, PLAIN, P], F32, name="sums", offset=0)
-        for lo, hi in ((0, PLAIN - 1), (PLAIN - 1, PLAIN)):
+        down = ps.tile([P, PLAIN, P], F32, name="down", tag=first_spread_tag)
+        for k in range(PLAIN):
+            nc.tensor.transpose(down[:, k, :], picked[:, k * P : (k + 1) * P], ident[:])
+        sums = sb.tile([P, PLAIN, P], F32, name="sums", tag="obs")
+        for lo, hi in RETURNS:
             up = ps.tile([P, hi - lo, P], F32, name="up%d" % lo)
-            for c in range(lo, hi):
-                nc.scalar.activation(sums[:, c, :], down[:, c, :], IDENT, bias=bias[:, c : c + 1])
-                nc.tensor.transpose(up[:, c - lo, :], sums[:, c, :], ident[:])
-            nc.scalar.copy(s[:, lo * P : hi * P], up[:].rearrange("q c p -> q (c p)"))
+            for k in range(lo, hi):
+                nc.scalar.activation(sums[:, k, :], down[:, k, :], IDENTITY, bias=plain_cols[:, k : k + 1])
+                nc.tensor.transpose(up[:, k - lo, :], sums[:, k, :], ident[:])
+            nc.scalar.copy(s[:, lo * P : hi * P], up[:].rearrange("q k p -> q (k p)"))
         s4 = s[:].rearrange("q (g r) -> q g r", r=R)
 
-        got_words = sb.tile([P, G], U32, name="got_words", tag="row%d" % FUSED[-1][0], align_bytes=64)
-        got_scales = sb.tile([P, G], U8, name="got_scales", tag="row%d" % FUSED[-2][0], align_bytes=64)
+        got_words = sb.tile([P, G], U32, name="got_words", tag=last_row_tag, align_bytes=64)
+        got_scales = sb.tile([P, G], U8, name="got_scales", tag="cum", align_bytes=64)
         obs_codes = sb.tile([P, Q], U32, name="obs_codes", align_bytes=64)
         obs_scales = sb.tile([P, Q], U8, name="obs_scales", align_bytes=64)
+        nc.vector.quantize_mx(
+            out=obs_codes[:].bitcast(FP8X4), scales=obs_scales[:], in_=obs_bf[:].rearrange("p q j -> p (q j)")
+        )
         nc.vector.tensor_copy(got_scales[:], scales[:].indirect(offs_sb[:]))
         nc.vector.tensor_copy(got_words[:], words[:].bitcast(U32).indirect(offs_sb[:]))
 
         pair_a = sb.tile([P, HG, 2], F32, name="pair_a")
-        pair_b = shared.tile([P, HG, 2], F32, name="pair_b", offset=0)
+        pair_b = sb.tile([P, HG, 2], F32, name="pair_b", tag="obs")
         best_a = sb.tile([P, HG], F32, name="best_a")
         best_b = sb.tile([P, HG], F32, name="best_b")
-        nc.vector.quantize_mx(
-            out=obs_codes[:].bitcast(FP8X4), scales=obs_scales[:], in_=obs_bf[:].rearrange("p q j -> p (q j)")
-        )
 
-        emis = ps.tile([P, G], F32, name="emis", tag="spread%d" % FUSED[0][0])
+        emis = ps.tile([P, G], F32, name="emis", tag=first_spread_tag)
         nc.tensor.matmul_mx(
             out=emis[:],
             lhsT=obs_codes[:].bitcast(FP8X4),
@@ -144,6 +137,7 @@ def tile_attend_viterbistep_kernel(tc, obs, emit_words, emit_scales, cum, step, 
         nc.vector.tensor_tensor(pair_a[:], s4[:, 0:HG, 0:2], s4[:, 0:HG, 2:4], MAX)
         nc.vector.tensor_tensor(best_b[:], pair_b[:, :, 0], pair_b[:, :, 1], MAX)
         nc.vector.tensor_tensor(best_a[:], pair_a[:, :, 0], pair_a[:, :, 1], MAX)
+
         res_a = sb.tile([P, HG], F32, name="res_a")
         res_b = sb.tile([P, HG], F32, name="res_b")
         nc.vector.tensor_tensor(res_b[:], emis[:, HG:G], best_b[:], ADD)

@@ -33,15 +33,16 @@ def tile_attend_viterbistep_kernel(tc, obs, emit_words, emit_scales, cum, step, 
     nc = tc.nc
     with ExitStack() as ctx:
         sb = ctx.enter_context(tc.tile_pool(name="sb", bufs=1))
+        shared = ctx.enter_context(tc.tile_pool(name="shared", bufs=1))
         ps = ctx.enter_context(tc.psum_pool(name="ps", bufs=1))
 
         def entries(lo, hi):
             return offs2_sb[:, lo * P // LIST_ROWS : hi * P // LIST_ROWS]
 
-        cum_sb = sb.tile([P, U], F32, name="cum_sb", tag="cum", align_bytes=64)
+        cum_sb = sb.tile([P, U], F32, name="cum_sb")
         offs2_sb = sb.tile([P, I // LIST_ROWS], U16, name="offs2_sb")
         offs_sb = sb.tile([P, G // LIST_ROWS], U16, name="offs_sb")
-        obs_sb = sb.tile([P, PACK, Q], F32, name="obs_sb", tag="obs")
+        obs_sb = shared.tile([P, PACK, Q], F32, name="obs_sb", offset=0)
         words = sb.tile([P, T], I32, name="words")
         scales = sb.tile([P, T], U8, name="scales")
         step_rows = sb.tile([P, P], F32, name="step_rows")
@@ -98,7 +99,7 @@ def tile_attend_viterbistep_kernel(tc, obs, emit_words, emit_scales, cum, step, 
         down = ps.tile([P, PLAIN, P], F32, name="down", tag=first_spread_tag)
         for k in range(PLAIN):
             nc.tensor.transpose(down[:, k, :], picked[:, k * P : (k + 1) * P], ident[:])
-        sums = sb.tile([P, PLAIN, P], F32, name="sums", tag="obs")
+        sums = shared.tile([P, PLAIN, P], F32, name="sums", offset=0)
         for lo, hi in RETURNS:
             up = ps.tile([P, hi - lo, P], F32, name="up%d" % lo)
             for k in range(lo, hi):
@@ -108,7 +109,7 @@ def tile_attend_viterbistep_kernel(tc, obs, emit_words, emit_scales, cum, step, 
         s4 = s[:].rearrange("q (g r) -> q g r", r=R)
 
         got_words = sb.tile([P, G], U32, name="got_words", tag=last_row_tag, align_bytes=64)
-        got_scales = sb.tile([P, G], U8, name="got_scales", tag="cum", align_bytes=64)
+        got_scales = shared.tile([P, G], U8, name="got_scales", offset=PLAIN * P * 4, align_bytes=64)
         obs_codes = sb.tile([P, Q], U32, name="obs_codes", align_bytes=64)
         obs_scales = sb.tile([P, Q], U8, name="obs_scales", align_bytes=64)
         nc.vector.quantize_mx(
@@ -118,7 +119,7 @@ def tile_attend_viterbistep_kernel(tc, obs, emit_words, emit_scales, cum, step, 
         nc.vector.tensor_copy(got_words[:], words[:].bitcast(U32).indirect(offs_sb[:]))
 
         pair_a = sb.tile([P, HG, 2], F32, name="pair_a")
-        pair_b = sb.tile([P, HG, 2], F32, name="pair_b", tag="obs")
+        pair_b = shared.tile([P, HG, 2], F32, name="pair_b", offset=0)
         best_a = sb.tile([P, HG], F32, name="best_a")
         best_b = sb.tile([P, HG], F32, name="best_b")
 

@@ -45,7 +45,7 @@ def tile_attend_viterbistep_kernel(tc, obs, emit_words, emit_scales, cum, step, 
         obs_sb = shared.tile([P, PACK, Q], F32, name="obs_sb", offset=0)
         words = sb.tile([P, T], I32, name="words")
         scales = sb.tile([P, T], U8, name="scales")
-        step_rows = sb.tile([P, P], F32, name="step_rows")
+        step_rows = sb.tile([P, P], F32, name="step_rows", tag="step_rows")
         ident = sb.tile([P, P], F32, name="ident")
 
         nc.gpsimd.memset(scales[:].bitcast(I32), 0)
@@ -68,7 +68,7 @@ def tile_attend_viterbistep_kernel(tc, obs, emit_words, emit_scales, cum, step, 
         turned = ps.tile([P, P], F32, name="turned")
         nc.tensor.transpose(turned[:], step_rows[:], ident[:])
         fused_cols = sb.tile([P, STRIPS - PLAIN], F32, name="fused_cols", tag="fused_cols", align_bytes=64)
-        nc.scalar.copy(fused_cols[:], turned[:, top + PLAIN : P])
+        nc.vector.tensor_copy(fused_cols[:], turned[:, top + PLAIN : P])
         plain_cols = sb.tile([P, PLAIN], F32, name="plain_cols")
         nc.scalar.copy(plain_cols[:], turned[:, top : top + PLAIN])
 
@@ -84,7 +84,7 @@ def tile_attend_viterbistep_kernel(tc, obs, emit_words, emit_scales, cum, step, 
         first_spread_tag = "spread%d" % FUSED[0][0]
         last_row_tag = "row%d" % FUSED[-1][0]
 
-        picked = sb.tile([P, PLAIN * P], F32, name="picked")
+        picked = sb.tile([P, PLAIN * P], F32, name="picked", tag="step_rows")
         s = sb.tile([P, I], F32, name="s")
         nc.vector.tensor_copy(picked[:], cum_sb[:].indirect(entries(0, PLAIN)))
         for (lo, hi), row in zip(FUSED, rows):
@@ -135,13 +135,16 @@ def tile_attend_viterbistep_kernel(tc, obs, emit_words, emit_scales, cum, step, 
         )
 
         nc.vector.tensor_tensor(pair_b[:], s4[:, HG:G, 0:2], s4[:, HG:G, 2:4], MAX)
-        nc.vector.tensor_tensor(pair_a[:], s4[:, 0:HG, 0:2], s4[:, 0:HG, 2:4], MAX)
-        nc.vector.tensor_tensor(best_b[:], pair_b[:, :, 0], pair_b[:, :, 1], MAX)
-        nc.vector.tensor_tensor(best_a[:], pair_a[:, :, 0], pair_a[:, :, 1], MAX)
+        quarters = (slice(0, HG // 2), slice(HG // 2, HG))
+        for part in quarters:
+            nc.vector.tensor_tensor(pair_a[:, part, :], s4[:, part, 0:2], s4[:, part, 2:4], MAX)
+        for best, pair in ((best_b, pair_b), (best_a, pair_a)):
+            for part in quarters:
+                nc.vector.tensor_tensor(best[:, part], pair[:, part, 0], pair[:, part, 1], MAX)
 
         res_a = sb.tile([P, HG], F32, name="res_a")
         res_b = sb.tile([P, HG], F32, name="res_b")
-        nc.vector.tensor_tensor(res_b[:], emis[:, HG:G], best_b[:], ADD)
-        nc.scalar.dma_start(out=out[:, HG:G], in_=res_b[:])
-        nc.vector.tensor_tensor(res_a[:], emis[:, 0:HG], best_a[:], ADD)
-        nc.sync.dma_start(out=out[:, 0:HG], in_=res_a[:])
+        for res, best, first, queue in ((res_b, best_b, HG, nc.scalar), (res_a, best_a, 0, nc.sync)):
+            for part in quarters:
+                nc.vector.tensor_tensor(res[:, part], emis[:, first + part.start : first + part.stop], best[:, part], ADD)
+            queue.dma_start(out=out[:, first : first + HG], in_=res[:])

@@ -25,7 +25,7 @@ R = I // G
 HG = G // 2
 STRIPS = I // P
 PLAIN = 3
-FUSED = ((PLAIN, PLAIN + 2), (PLAIN + 2, STRIPS))
+FUSED = ((PLAIN, PLAIN + 1), (PLAIN + 1, PLAIN + 3), (PLAIN + 3, STRIPS))
 RETURNS = ((0, PLAIN - 1), (PLAIN - 1, PLAIN))
 
 
@@ -90,7 +90,7 @@ def tile_attend_viterbistep_kernel(tc, obs, emit_words, emit_scales, cum, step, 
         for (lo, hi), row in zip(FUSED, rows):
             nc.vector.tensor_tensor(s[:, lo * P : hi * P], cum_sb[:].indirect(entries(lo, hi)), row[:], ADD)
 
-        obs_bf = sb.tile([P, Q, PACK], BF16, name="obs_bf", tag="fused_cols", align_bytes=64)
+        obs_bf = sb.tile([P, Q, PACK], BF16, name="obs_bf", tag="row%d" % FUSED[0][0], align_bytes=64)
         nc.scalar.copy(
             obs_bf[:].rearrange("p (c i) j -> p c j i", i=4),
             obs_sb[:].rearrange("p j (c i) -> p c j i", i=4),
@@ -108,7 +108,7 @@ def tile_attend_viterbistep_kernel(tc, obs, emit_words, emit_scales, cum, step, 
             nc.scalar.copy(s[:, lo * P : hi * P], up[:].rearrange("q k p -> q (k p)"))
         s4 = s[:].rearrange("q (g r) -> q g r", r=R)
 
-        got_words = sb.tile([P, G], U32, name="got_words", tag=last_row_tag, align_bytes=64)
+        got_words = shared.tile([P, G], U32, name="got_words", offset=PLAIN * P * 4 + G, align_bytes=64)
         got_scales = shared.tile([P, G], U8, name="got_scales", offset=PLAIN * P * 4, align_bytes=64)
         obs_codes = sb.tile([P, Q], U32, name="obs_codes", align_bytes=64)
         obs_scales = sb.tile([P, Q], U8, name="obs_scales", align_bytes=64)

@@ -45,7 +45,7 @@ def tile_attend_viterbistep_kernel(tc, obs, emit_words, emit_scales, cum, step, 
         obs_sb = shared.tile([P, PACK, Q], F32, name="obs_sb", offset=0)
         words = sb.tile([P, T], I32, name="words")
         scales = sb.tile([P, T], U8, name="scales")
-        step_rows = sb.tile([P, P], F32, name="step_rows", tag="step_rows")
+        step_rows = sb.tile([P, P], F32, name="step_rows", tag="step_rows", align_bytes=64)
         ident = sb.tile([P, P], F32, name="ident")
 
         nc.gpsimd.memset(scales[:].bitcast(I32), 0)
@@ -84,7 +84,7 @@ def tile_attend_viterbistep_kernel(tc, obs, emit_words, emit_scales, cum, step, 
         first_spread_tag = "spread%d" % FUSED[0][0]
         last_row_tag = "row%d" % FUSED[-1][0]
 
-        picked = sb.tile([P, PLAIN * P], F32, name="picked", tag="step_rows")
+        picked = sb.tile([P, PLAIN * P], F32, name="picked", tag="step_rows", align_bytes=64)
         s = sb.tile([P, I], F32, name="s")
         nc.vector.tensor_copy(picked[:], cum_sb[:].indirect(entries(0, PLAIN)))
         for (lo, hi), row in zip(FUSED, rows):
@@ -109,13 +109,13 @@ def tile_attend_viterbistep_kernel(tc, obs, emit_words, emit_scales, cum, step, 
         s4 = s[:].rearrange("q (g r) -> q g r", r=R)
 
         got_words = shared.tile([P, G], U32, name="got_words", offset=PLAIN * P * 4 + G, align_bytes=64)
-        got_scales = shared.tile([P, G], U8, name="got_scales", offset=PLAIN * P * 4, align_bytes=64)
+        got_scales = sb.tile([P, G], U8, name="got_scales", tag="step_rows", align_bytes=64)
         obs_codes = sb.tile([P, Q], U32, name="obs_codes", align_bytes=64)
         obs_scales = sb.tile([P, Q], U8, name="obs_scales", align_bytes=64)
+        nc.vector.tensor_copy(got_scales[:], scales[:].indirect(offs_sb[:]))
         nc.vector.quantize_mx(
             out=obs_codes[:].bitcast(FP8X4), scales=obs_scales[:], in_=obs_bf[:].rearrange("p q j -> p (q j)")
         )
-        nc.vector.tensor_copy(got_scales[:], scales[:].indirect(offs_sb[:]))
         nc.vector.tensor_copy(got_words[:], words[:].bitcast(U32).indirect(offs_sb[:]))
 
         pair_a = sb.tile([P, HG, 2], F32, name="pair_a")

@@ -15,7 +15,7 @@ U8 = mybir.dt.uint8
 FP8X4 = mybir.dt.float8_e4m3fn_x4
 ADD = mybir.AluOpType.add
 MAX = mybir.AluOpType.max
-IDENTITY = mybir.ActivationFunctionType.Identity
+COPY = mybir.ActivationFunctionType.Copy
 
 P = 128
 PACK = 4
@@ -24,9 +24,8 @@ LIST_ROWS = 16
 R = I // G
 HG = G // 2
 STRIPS = I // P
-PLAIN = 3
-FUSED = ((PLAIN, PLAIN + 1), (PLAIN + 1, PLAIN + 3), (PLAIN + 3, STRIPS))
-RETURNS = ((0, PLAIN - 1), (PLAIN - 1, PLAIN))
+PIECE = 2 * P
+PIECES = I // PIECE
 
 
 def tile_attend_viterbistep_kernel(tc, obs, emit_words, emit_scales, cum, step, offs, offs2, out):
@@ -36,16 +35,14 @@ def tile_attend_viterbistep_kernel(tc, obs, emit_words, emit_scales, cum, step, 
         shared = ctx.enter_context(tc.tile_pool(name="shared", bufs=1))
         ps = ctx.enter_context(tc.psum_pool(name="ps", bufs=1))
 
-        def entries(lo, hi):
-            return offs2_sb[:, lo * P // LIST_ROWS : hi * P // LIST_ROWS]
-
-        cum_sb = sb.tile([P, U], F32, name="cum_sb")
+        late = ctx.enter_context(tc.tile_pool(name="late", bufs=1))
+        cum_sb = late.tile([P, U], F32, name="cum_sb", offset=0, align_bytes=64)
         offs2_sb = sb.tile([P, I // LIST_ROWS], U16, name="offs2_sb")
         offs_sb = sb.tile([P, G // LIST_ROWS], U16, name="offs_sb")
-        obs_sb = shared.tile([P, PACK, Q], F32, name="obs_sb", offset=0)
+        obs_sb = late.tile([P, PACK, Q], F32, name="obs_sb", offset=U * 4, align_bytes=64)
         words = sb.tile([P, T], I32, name="words")
         scales = sb.tile([P, T], U8, name="scales")
-        step_rows = sb.tile([P, P], F32, name="step_rows", tag="step_rows", align_bytes=64)
+        step_rows = shared.tile([P, P], F32, name="step_rows", offset=0)
         ident = sb.tile([P, P], F32, name="ident")
 
         nc.gpsimd.memset(scales[:].bitcast(I32), 0)
@@ -67,84 +64,82 @@ def tile_attend_viterbistep_kernel(tc, obs, emit_words, emit_scales, cum, step, 
 
         turned = ps.tile([P, P], F32, name="turned")
         nc.tensor.transpose(turned[:], step_rows[:], ident[:])
-        fused_cols = sb.tile([P, STRIPS - PLAIN], F32, name="fused_cols", tag="fused_cols", align_bytes=64)
-        nc.vector.tensor_copy(fused_cols[:], turned[:, top + PLAIN : P])
-        plain_cols = sb.tile([P, PLAIN], F32, name="plain_cols")
-        nc.scalar.copy(plain_cols[:], turned[:, top : top + PLAIN])
+        cols = sb.tile([P, STRIPS], F32, name="cols", tag="cols", align_bytes=64)
+        nc.scalar.activation(cols[:], turned[:, top:P], COPY)
+        spreads = []
+        for n in range(PIECES):
+            spread = ps.tile([P, PIECE], F32, name="spread%d" % n)
+            for k in range(2):
+                column = cols[:, 2 * n + k : 2 * n + k + 1]
+                nc.tensor.transpose(spread[:, k * P : (k + 1) * P], column.to_broadcast([P, P]), ident[:])
+            spreads.append(spread)
 
-        rows = []
-        for lo, hi in FUSED:
-            spread = ps.tile([P, hi - lo, P], F32, name="spread%d" % lo, tag="spread%d" % lo)
-            for k in range(lo, hi):
-                column = fused_cols[:, k - PLAIN : k - PLAIN + 1]
-                nc.tensor.transpose(spread[:, k - lo, :], column.to_broadcast([P, P]), ident[:])
-            row = sb.tile([P, (hi - lo) * P], F32, name="row%d" % lo, tag="row%d" % lo, align_bytes=64)
-            nc.scalar.copy(row[:], spread[:].rearrange("q k p -> q (k p)"))
-            rows.append(row)
-        first_spread_tag = "spread%d" % FUSED[0][0]
-        last_row_tag = "row%d" % FUSED[-1][0]
+        def entries(n):
+            return offs2_sb[:, n * PIECE // LIST_ROWS : (n + 1) * PIECE // LIST_ROWS]
 
-        picked = sb.tile([P, PLAIN * P], F32, name="picked", tag="step_rows", align_bytes=64)
+        first = sb.tile([P, PIECE], F32, name="first")
+        rest = shared.tile([P, PIECES - 1, PIECE], F32, name="rest", offset=0)
+        picked = [first[:]] + [rest[:, n, :] for n in range(PIECES - 1)]
         s = sb.tile([P, I], F32, name="s")
-        nc.vector.tensor_copy(picked[:], cum_sb[:].indirect(entries(0, PLAIN)))
-        for (lo, hi), row in zip(FUSED, rows):
-            nc.vector.tensor_tensor(s[:, lo * P : hi * P], cum_sb[:].indirect(entries(lo, hi)), row[:], ADD)
+        s4 = s[:].rearrange("q (g r) -> q g r", r=R)
+        nc.vector.tensor_copy(picked[0], cum_sb[:].indirect(entries(0)))
+        for n in range(1, PIECES):
+            nc.scalar.activation(picked[n], cum_sb[:].indirect(entries(n)), COPY)
 
-        obs_bf = sb.tile([P, Q, PACK], BF16, name="obs_bf", tag="row%d" % FUSED[0][0], align_bytes=64)
+        def add_step(n):
+            nc.vector.tensor_tensor(s[:, n * PIECE : (n + 1) * PIECE], picked[n], spreads[n][:], ADD)
+
+        def larger_pairs(h, pair):
+            half = slice(h * HG, (h + 1) * HG)
+            nc.vector.tensor_tensor(pair[:], s4[:, half, 0:2], s4[:, half, 2:4], MAX)
+
+        add_step(0)
+        add_step(1)
+        pair_a = sb.tile([P, HG, 2], F32, name="pair_a")
+        larger_pairs(0, pair_a)
+        add_step(2)
+        got_scales = sb.tile([P, G], U8, name="got_scales", tag="cols", align_bytes=64)
+        nc.vector.tensor_copy(got_scales[:], scales[:].indirect(offs_sb[:]))
+        add_step(3)
+
+        obs_bf = late.tile([P, Q, PACK], BF16, name="obs_bf", offset=0, align_bytes=64)
         nc.scalar.copy(
             obs_bf[:].rearrange("p (c i) j -> p c j i", i=4),
             obs_sb[:].rearrange("p j (c i) -> p c j i", i=4),
         )
-
-        down = ps.tile([P, PLAIN, P], F32, name="down", tag=first_spread_tag)
-        for k in range(PLAIN):
-            nc.tensor.transpose(down[:, k, :], picked[:, k * P : (k + 1) * P], ident[:])
-        sums = shared.tile([P, PLAIN, P], F32, name="sums", offset=0)
-        for lo, hi in RETURNS:
-            up = ps.tile([P, hi - lo, P], F32, name="up%d" % lo)
-            for k in range(lo, hi):
-                nc.scalar.activation(sums[:, k, :], down[:, k, :], IDENTITY, bias=plain_cols[:, k : k + 1])
-                nc.tensor.transpose(up[:, k - lo, :], sums[:, k, :], ident[:])
-            nc.scalar.copy(s[:, lo * P : hi * P], up[:].rearrange("q k p -> q (k p)"))
-        s4 = s[:].rearrange("q (g r) -> q g r", r=R)
-
-        got_words = shared.tile([P, G], U32, name="got_words", offset=PLAIN * P * 4 + G, align_bytes=64)
-        got_scales = sb.tile([P, G], U8, name="got_scales", tag="step_rows", align_bytes=64)
         obs_codes = sb.tile([P, Q], U32, name="obs_codes", align_bytes=64)
         obs_scales = sb.tile([P, Q], U8, name="obs_scales", align_bytes=64)
-        nc.vector.tensor_copy(got_scales[:], scales[:].indirect(offs_sb[:]))
         nc.vector.quantize_mx(
             out=obs_codes[:].bitcast(FP8X4), scales=obs_scales[:], in_=obs_bf[:].rearrange("p q j -> p (q j)")
         )
-        nc.vector.tensor_copy(got_words[:], words[:].bitcast(U32).indirect(offs_sb[:]))
 
-        pair_a = sb.tile([P, HG, 2], F32, name="pair_a")
-        pair_b = shared.tile([P, HG, 2], F32, name="pair_b", offset=0)
-        best_a = sb.tile([P, HG], F32, name="best_a")
-        best_b = sb.tile([P, HG], F32, name="best_b")
+        sums = []
+        for h in range(2):
+            got_words = late.tile([P, HG], U32, name="got_words%d" % h, offset=(U + HG // 2 + h * HG) * 4, align_bytes=64)
+            listed = offs_sb[:, h * HG // LIST_ROWS : (h + 1) * HG // LIST_ROWS]
+            nc.vector.tensor_copy(got_words[:], words[:].bitcast(U32).indirect(listed))
+            emis = ps.tile([P, HG], F32, name="emis%d" % h)
+            nc.tensor.matmul_mx(
+                out=emis[:],
+                lhsT=obs_codes[:].bitcast(FP8X4),
+                lhsT_scale=obs_scales[:],
+                rhs=got_words[:].bitcast(FP8X4),
+                rhs_scale=got_scales[:, h * HG : (h + 1) * HG],
+                start=True,
+                stop=True,
+            )
+            sums.append(emis)
 
-        emis = ps.tile([P, G], F32, name="emis", tag=first_spread_tag)
-        nc.tensor.matmul_mx(
-            out=emis[:],
-            lhsT=obs_codes[:].bitcast(FP8X4),
-            lhsT_scale=obs_scales[:],
-            rhs=got_words[:].bitcast(FP8X4),
-            rhs_scale=got_scales[:],
-            start=True,
-            stop=True,
-        )
+        pair_b = late.tile([P, HG, 2], F32, name="pair_b", offset=(U + HG // 2 + G) * 4, align_bytes=64)
+        larger_pairs(1, pair_b)
+        bests = [
+            late.tile([P, HG], F32, name="best_a", offset=(U - HG // 2) * 4, align_bytes=64),
+            sb.tile([P, HG], F32, name="best_b"),
+        ]
+        for best, pair in zip(bests, (pair_a, pair_b)):
+            nc.vector.tensor_tensor(best[:], pair[:, :, 0], pair[:, :, 1], MAX)
 
-        nc.vector.tensor_tensor(pair_b[:], s4[:, HG:G, 0:2], s4[:, HG:G, 2:4], MAX)
-        quarters = (slice(0, HG // 2), slice(HG // 2, HG))
-        for part in quarters:
-            nc.vector.tensor_tensor(pair_a[:, part, :], s4[:, part, 0:2], s4[:, part, 2:4], MAX)
-        for best, pair in ((best_b, pair_b), (best_a, pair_a)):
-            for part in quarters:
-                nc.vector.tensor_tensor(best[:, part], pair[:, part, 0], pair[:, part, 1], MAX)
-
-        res_a = sb.tile([P, HG], F32, name="res_a")
-        res_b = sb.tile([P, HG], F32, name="res_b")
-        for res, best, first, queue in ((res_b, best_b, HG, nc.scalar), (res_a, best_a, 0, nc.sync)):
-            for part in quarters:
-                nc.vector.tensor_tensor(res[:, part], emis[:, first + part.start : first + part.stop], best[:, part], ADD)
-            queue.dma_start(out=out[:, first : first + HG], in_=res[:])
+        for h, queue in ((0, nc.scalar), (1, nc.sync)):
+            res = sb.tile([P, HG], F32, name="res%d" % h)
+            nc.vector.tensor_tensor(res[:], sums[h][:], bests[h][:], ADD)
+            queue.dma_start(out=out[:, h * HG : (h + 1) * HG], in_=res[:])

@@ -15,6 +15,7 @@ U8 = mybir.dt.uint8
 FP8X4 = mybir.dt.float8_e4m3fn_x4
 ADD = mybir.AluOpType.add
 MAX = mybir.AluOpType.max
+IDENTITY = mybir.ActivationFunctionType.Identity
 COPY = mybir.ActivationFunctionType.Copy
 
 P = 128
@@ -26,6 +27,8 @@ HG = G // 2
 STRIPS = I // P
 PIECE = 2 * P
 PIECES = I // PIECE
+SPLIT = 3 * P
+BANK = 512
 
 
 def tile_attend_viterbistep_kernel(tc, obs, emit_words, emit_scales, cum, step, offs, offs2, out):
@@ -35,22 +38,24 @@ def tile_attend_viterbistep_kernel(tc, obs, emit_words, emit_scales, cum, step, 
         shared = ctx.enter_context(tc.tile_pool(name="shared", bufs=1))
         ps = ctx.enter_context(tc.psum_pool(name="ps", bufs=1))
 
+        ps_shared = ctx.enter_context(tc.psum_pool(name="ps_shared", bufs=1))
+        mid = ctx.enter_context(tc.tile_pool(name="mid", bufs=1))
         late = ctx.enter_context(tc.tile_pool(name="late", bufs=1))
-        cum_sb = late.tile([P, U], F32, name="cum_sb", offset=0, align_bytes=64)
+        cum_sb = sb.tile([P, U], F32, name="cum_sb")
         offs2_sb = sb.tile([P, I // LIST_ROWS], U16, name="offs2_sb")
         offs_sb = sb.tile([P, G // LIST_ROWS], U16, name="offs_sb")
-        obs_sb = late.tile([P, PACK, Q], F32, name="obs_sb", offset=U * 4, align_bytes=64)
+        obs_sb = shared.tile([P, PACK, Q], F32, name="obs_sb", offset=I * 4)
         words = sb.tile([P, T], I32, name="words")
         scales = sb.tile([P, T], U8, name="scales")
-        step_rows = shared.tile([P, P], F32, name="step_rows", offset=0)
+        step_rows = shared.tile([P, PIECE], F32, name="step_rows", offset=0)
         ident = sb.tile([P, P], F32, name="ident")
 
         nc.gpsimd.memset(scales[:].bitcast(I32), 0)
-        top = P - STRIPS
+        top = P - PIECES
         nc.vector.memset(step_rows[0:top, :], 0.0)
 
         nc.sync.dma_start(offs2_sb[:], offs2)
-        nc.scalar.dma_start(out=step_rows[top:P, :], in_=step[0].rearrange("(k j) -> k j", j=P))
+        nc.scalar.dma_start(out=step_rows[top:P, :], in_=step[0].rearrange("(n j) -> n j", j=PIECE))
         nc.sync.dma_start(out=cum_sb[:], in_=cum)
         nc.sync.dma_start(out=obs_sb[:], in_=obs.rearrange("(p j) q -> p j q", j=PACK))
         nc.sync.dma_start(offs_sb[:], offs)
@@ -62,84 +67,90 @@ def tile_attend_viterbistep_kernel(tc, obs, emit_words, emit_scales, cum, step, 
 
         make_identity(nc, ident[:])
 
-        turned = ps.tile([P, P], F32, name="turned")
-        nc.tensor.transpose(turned[:], step_rows[:], ident[:])
-        cols = sb.tile([P, STRIPS], F32, name="cols", tag="cols", align_bytes=64)
-        nc.scalar.activation(cols[:], turned[:, top:P], COPY)
+        turned = ps_shared.tile([P, 2, BANK], F32, name="turned", offset=0)
+        for e in range(2):
+            nc.tensor.transpose(turned[:, 0, e * P : (e + 1) * P], step_rows[:, e:PIECE:2], ident[:])
+        columns = turned[:, 0, 0 : 2 * P].rearrange("p (e n) -> p e n", e=2)
+        spread_room = mid.tile([P, 4, 4], F32, name="spread_room", offset=G - 32)
+        spread_cols = spread_room[:, 0:2, 0:2]
+        even_room = late.tile([P, 3 * P], F32, name="even_room", offset=0, align_bytes=64)
+        odd = sb.tile([P, 2], F32, name="odd")
+        nc.scalar.activation(spread_cols, columns[:, :, top + 2 : P], COPY)
+        nc.scalar.activation(even_room[:, 0:2], columns[:, 0, top : top + 2], COPY)
+        nc.scalar.activation(odd[:], columns[:, 1, top : top + 2], COPY)
         spreads = []
-        for n in range(PIECES):
-            spread = ps.tile([P, PIECE], F32, name="spread%d" % n)
-            for k in range(2):
-                column = cols[:, 2 * n + k : 2 * n + k + 1]
-                nc.tensor.transpose(spread[:, k * P : (k + 1) * P], column.to_broadcast([P, P]), ident[:])
-            spreads.append(spread)
+        for n in range(2):
+            spread = ps.tile([P, 2, P], F32, name="spread%d" % n)
+            for e in range(2):
+                nc.tensor.transpose(spread[:, e, :], spread_cols[:, e, n : n + 1].to_broadcast([P, P]), ident[:])
+            spreads.append(spread[:].rearrange("q e p -> q p e"))
 
-        def entries(n):
-            return offs2_sb[:, n * PIECE // LIST_ROWS : (n + 1) * PIECE // LIST_ROWS]
+        def entries(lo, hi):
+            return offs2_sb[:, lo // LIST_ROWS : hi // LIST_ROWS]
 
-        first = sb.tile([P, PIECE], F32, name="first")
-        rest = shared.tile([P, PIECES - 1, PIECE], F32, name="rest", offset=0)
-        picked = [first[:]] + [rest[:, n, :] for n in range(PIECES - 1)]
-        s = sb.tile([P, I], F32, name="s")
-        s4 = s[:].rearrange("q (g r) -> q g r", r=R)
-        nc.vector.tensor_copy(picked[0], cum_sb[:].indirect(entries(0)))
-        for n in range(1, PIECES):
-            nc.scalar.activation(picked[n], cum_sb[:].indirect(entries(n)), COPY)
+        picked = shared.tile([P, I], F32, name="picked", offset=0)
+        nc.vector.tensor_copy(picked[:, 0:SPLIT], cum_sb[:].indirect(entries(0, SPLIT)))
+        for lo, hi in ((2 * PIECE, 3 * PIECE), (3 * PIECE, I), (SPLIT, 2 * PIECE)):
+            nc.scalar.activation(picked[:, lo:hi], cum_sb[:].indirect(entries(lo, hi)), COPY)
 
-        def add_step(n):
-            nc.vector.tensor_tensor(s[:, n * PIECE : (n + 1) * PIECE], picked[n], spreads[n][:], ADD)
-
-        def larger_pairs(h, pair):
-            half = slice(h * HG, (h + 1) * HG)
-            nc.vector.tensor_tensor(pair[:], s4[:, half, 0:2], s4[:, half, 2:4], MAX)
-
-        add_step(0)
-        add_step(1)
-        pair_a = sb.tile([P, HG, 2], F32, name="pair_a")
-        larger_pairs(0, pair_a)
-        add_step(2)
-        got_scales = sb.tile([P, G], U8, name="got_scales", tag="cols", align_bytes=64)
-        nc.vector.tensor_copy(got_scales[:], scales[:].indirect(offs_sb[:]))
-        add_step(3)
-
-        obs_bf = late.tile([P, Q, PACK], BF16, name="obs_bf", offset=0, align_bytes=64)
+        obs_bf = mid.tile([P, Q, PACK], BF16, name="obs_bf", offset=G, align_bytes=64)
         nc.scalar.copy(
             obs_bf[:].rearrange("p (c i) j -> p c j i", i=4),
             obs_sb[:].rearrange("p j (c i) -> p c j i", i=4),
         )
+
+        s = sb.tile([P, 2, P, 2], F32, name="s")
+        for n in range(2):
+            piece = picked[:, (2 + n) * PIECE : (3 + n) * PIECE].rearrange("q (p e) -> q p e", e=2)
+            nc.vector.tensor_tensor(s[:, n, :, :], piece, spreads[n], ADD)
+        s4 = s[:].rearrange("q n (g x) e -> q (n g) (x e)", x=2)
+        got_scales = mid.tile([P, G], U8, name="got_scales", offset=0, align_bytes=64)
+        nc.vector.tensor_copy(got_scales[:], scales[:].indirect(offs_sb[:]))
+        pair = sb.tile([P, HG, 2], F32, name="pair")
+        nc.vector.tensor_tensor(pair[:], s4[:, :, 0:2], s4[:, :, 2:4], MAX)
         obs_codes = sb.tile([P, Q], U32, name="obs_codes", align_bytes=64)
         obs_scales = sb.tile([P, Q], U8, name="obs_scales", align_bytes=64)
         nc.vector.quantize_mx(
             out=obs_codes[:].bitcast(FP8X4), scales=obs_scales[:], in_=obs_bf[:].rearrange("p q j -> p (q j)")
         )
 
+        down_a = ps_shared.tile([P, 2, P], F32, name="down_a", offset=0)
+        down_b = ps_shared.tile([P, 2, BANK], F32, name="down_b", offset=BANK * 4)
+        up = ps.tile([P, 2, P], F32, name="up")
+        for n, down in enumerate((down_a, down_b)):
+            for e in range(2):
+                nc.tensor.transpose(down[:, e, 0:P], picked[:, n * PIECE + e : (n + 1) * PIECE : 2], ident[:])
+        for n, down in enumerate((down_a, down_b)):
+            summed = shared.tile([P, P], F32, name="summed%d" % n, offset=(I + n * P) * 4)
+            nc.scalar.activation(summed[:], down[:, 0, 0:P], IDENTITY, bias=even_room[:, n : n + 1])
+            larger = shared.tile([P, P], F32, name="larger%d" % n, offset=(I + (2 + n) * P) * 4)
+            nc.vector.scalar_tensor_tensor(larger[:], down[:, 1, 0:P], odd[:, n : n + 1], summed[:], ADD, MAX)
+            nc.tensor.transpose(up[:, n, :], larger[:], ident[:])
+
         sums = []
         for h in range(2):
-            got_words = late.tile([P, HG], U32, name="got_words%d" % h, offset=(U + HG // 2 + h * HG) * 4, align_bytes=64)
-            listed = offs_sb[:, h * HG // LIST_ROWS : (h + 1) * HG // LIST_ROWS]
+            got_words = late.tile([P, HG], U32, name="got_words%d" % h, offset=h * HG * 4, align_bytes=64)
+            listed = offs_sb[:, (1 - h) * HG // LIST_ROWS : (2 - h) * HG // LIST_ROWS]
             nc.vector.tensor_copy(got_words[:], words[:].bitcast(U32).indirect(listed))
-            emis = ps.tile([P, HG], F32, name="emis%d" % h)
+            emis = ps_shared.tile([P, HG], F32, name="emis%d" % h, offset=(1 + h) * BANK * 4)
             nc.tensor.matmul_mx(
                 out=emis[:],
                 lhsT=obs_codes[:].bitcast(FP8X4),
                 lhsT_scale=obs_scales[:],
                 rhs=got_words[:].bitcast(FP8X4),
-                rhs_scale=got_scales[:, h * HG : (h + 1) * HG],
+                rhs_scale=got_scales[:, (1 - h) * HG : (2 - h) * HG],
                 start=True,
                 stop=True,
             )
             sums.append(emis)
 
-        pair_b = late.tile([P, HG, 2], F32, name="pair_b", offset=(U + HG // 2 + G) * 4, align_bytes=64)
-        larger_pairs(1, pair_b)
-        bests = [
-            late.tile([P, HG], F32, name="best_a", offset=(U - HG // 2) * 4, align_bytes=64),
-            sb.tile([P, HG], F32, name="best_b"),
-        ]
-        for best, pair in zip(bests, (pair_a, pair_b)):
-            nc.vector.tensor_tensor(best[:], pair[:, :, 0], pair[:, :, 1], MAX)
+        best_b = late.tile([P, HG], F32, name="best_b", offset=G * 4)
+        nc.vector.tensor_tensor(best_b[:], pair[:, :, 0], pair[:, :, 1], MAX)
+        best_a = sb.tile([P, HG], F32, name="best_a")
+        nc.vector.tensor_reduce(best_a[:], up[:].rearrange("q n (g r) -> q (n g) r", r=2), mybir.AxisListType.X, MAX)
+        bests = [best_b[:], best_a[:]]
 
         for h, queue in ((0, nc.scalar), (1, nc.sync)):
-            res = sb.tile([P, HG], F32, name="res%d" % h)
-            nc.vector.tensor_tensor(res[:], sums[h][:], bests[h][:], ADD)
-            queue.dma_start(out=out[:, h * HG : (h + 1) * HG], in_=res[:])
+            res = shared.tile([P, HG], F32, name="res%d" % h, offset=(I + (3 + h) * P) * 4)
+            nc.vector.tensor_tensor(res[:], sums[h][:], bests[h], ADD)
+            queue.dma_start(out=out[:, (1 - h) * HG : (2 - h) * HG], in_=res[:])

@@ -27,7 +27,7 @@ HG = G // 2
 STRIPS = I // P
 PIECE = 2 * P
 PIECES = I // PIECE
-SPLIT = 3 * P
+SPLIT = 7 * P // 2
 BANK = 512
 
 
@@ -69,27 +69,26 @@ def tile_attend_viterbistep_kernel(tc, obs, emit_words, emit_scales, cum, step, 
 
         turned = ps_shared.tile([P, 2, BANK], F32, name="turned", offset=0)
         for e in range(2):
-            nc.tensor.transpose(turned[:, 0, e * P : (e + 1) * P], step_rows[:, e:PIECE:2], ident[:])
-        columns = turned[:, 0, 0 : 2 * P].rearrange("p (e n) -> p e n", e=2)
-        spread_room = mid.tile([P, 4, 4], F32, name="spread_room", offset=G - 32)
-        spread_cols = spread_room[:, 0:2, 0:2]
+            nc.tensor.transpose(turned[:, e, 0:P], step_rows[:, e:PIECE:2], ident[:])
         even_room = late.tile([P, 3 * P], F32, name="even_room", offset=0, align_bytes=64)
+        spread_room = mid.tile([P, 16], F32, name="spread_room", offset=G - 32)
         odd = sb.tile([P, 2], F32, name="odd")
-        nc.scalar.activation(spread_cols, columns[:, :, top + 2 : P], COPY)
-        nc.scalar.activation(even_room[:, 0:2], columns[:, 0, top : top + 2], COPY)
-        nc.scalar.activation(odd[:], columns[:, 1, top : top + 2], COPY)
+        nc.scalar.activation(even_room[:, 0:PIECES], turned[:, 0, top:P], COPY)
+        nc.scalar.activation(spread_room[:, 0:2], turned[:, 1, top + 2 : P], COPY)
+        nc.scalar.activation(odd[:], turned[:, 1, top : top + 2], COPY)
         spreads = []
         for n in range(2):
             spread = ps.tile([P, 2, P], F32, name="spread%d" % n)
-            for e in range(2):
-                nc.tensor.transpose(spread[:, e, :], spread_cols[:, e, n : n + 1].to_broadcast([P, P]), ident[:])
+            for e, column in enumerate((even_room[:, 2 + n : 3 + n], spread_room[:, n : n + 1])):
+                nc.tensor.transpose(spread[:, e, :], column.to_broadcast([P, P]), ident[:])
             spreads.append(spread[:].rearrange("q e p -> q p e"))
 
         def entries(lo, hi):
             return offs2_sb[:, lo // LIST_ROWS : hi // LIST_ROWS]
 
         picked = shared.tile([P, I], F32, name="picked", offset=0)
-        nc.vector.tensor_copy(picked[:, 0:SPLIT], cum_sb[:].indirect(entries(0, SPLIT)))
+        for lo, hi in ((0, PIECE), (PIECE, SPLIT)):
+            nc.vector.tensor_copy(picked[:, lo:hi], cum_sb[:].indirect(entries(lo, hi)))
         for lo, hi in ((2 * PIECE, 3 * PIECE), (3 * PIECE, I), (SPLIT, 2 * PIECE)):
             nc.scalar.activation(picked[:, lo:hi], cum_sb[:].indirect(entries(lo, hi)), COPY)
 

@@ -27,7 +27,7 @@ HG = G // 2
 STRIPS = I // P
 PIECE = 2 * P
 PIECES = I // PIECE
-SPLIT = 7 * P // 2
+SPLIT = 5 * P // 2
 BANK = 512
 
 
@@ -87,9 +87,9 @@ def tile_attend_viterbistep_kernel(tc, obs, emit_words, emit_scales, cum, step, 
             return offs2_sb[:, lo // LIST_ROWS : hi // LIST_ROWS]
 
         picked = shared.tile([P, I], F32, name="picked", offset=0)
-        for lo, hi in ((0, PIECE), (PIECE, SPLIT)):
+        for lo, hi in ((0, SPLIT), (I - P, I)):
             nc.vector.tensor_copy(picked[:, lo:hi], cum_sb[:].indirect(entries(lo, hi)))
-        for lo, hi in ((2 * PIECE, 3 * PIECE), (3 * PIECE, I), (SPLIT, 2 * PIECE)):
+        for lo, hi in ((2 * PIECE, 3 * PIECE), (3 * PIECE, I - P), (SPLIT, 2 * PIECE)):
             nc.scalar.activation(picked[:, lo:hi], cum_sb[:].indirect(entries(lo, hi)), COPY)
 
         obs_bf = mid.tile([P, Q, PACK], BF16, name="obs_bf", offset=G, align_bytes=64)
@@ -103,10 +103,11 @@ def tile_attend_viterbistep_kernel(tc, obs, emit_words, emit_scales, cum, step, 
             piece = picked[:, (2 + n) * PIECE : (3 + n) * PIECE].rearrange("q (p e) -> q p e", e=2)
             nc.vector.tensor_tensor(s[:, n, :, :], piece, spreads[n], ADD)
         s4 = s[:].rearrange("q n (g x) e -> q (n g) (x e)", x=2)
+        pair = sb.tile([P, HG, 2], F32, name="pair")
+        for part in (slice(0, HG // 2), slice(HG // 2, HG)):
+            nc.vector.tensor_tensor(pair[:, part, :], s4[:, part, 0:2], s4[:, part, 2:4], MAX)
         got_scales = mid.tile([P, G], U8, name="got_scales", offset=0, align_bytes=64)
         nc.vector.tensor_copy(got_scales[:], scales[:].indirect(offs_sb[:]))
-        pair = sb.tile([P, HG, 2], F32, name="pair")
-        nc.vector.tensor_tensor(pair[:], s4[:, :, 0:2], s4[:, :, 2:4], MAX)
         obs_codes = sb.tile([P, Q], U32, name="obs_codes", align_bytes=64)
         obs_scales = sb.tile([P, Q], U8, name="obs_scales", align_bytes=64)
         nc.vector.quantize_mx(

@@ -27,7 +27,7 @@ HG = G // 2
 STRIPS = I // P
 PIECE = 2 * P
 PIECES = I // PIECE
-SPLIT = 5 * P // 2
+SPLIT = 2 * P
 BANK = 512
 
 
@@ -70,7 +70,7 @@ def tile_attend_viterbistep_kernel(tc, obs, emit_words, emit_scales, cum, step, 
         turned = ps_shared.tile([P, 2, BANK], F32, name="turned", offset=0)
         for e in range(2):
             nc.tensor.transpose(turned[:, e, 0:P], step_rows[:, e:PIECE:2], ident[:])
-        even_room = late.tile([P, 3 * P], F32, name="even_room", offset=0, align_bytes=64)
+        even_room = late.tile([P, 2 * P], F32, name="even_room", offset=0, align_bytes=64)
         spread_room = mid.tile([P, 16], F32, name="spread_room", offset=G - 32)
         odd = sb.tile([P, 2], F32, name="odd")
         nc.scalar.activation(even_room[:, 0:PIECES], turned[:, 0, top:P], COPY)
@@ -108,6 +108,8 @@ def tile_attend_viterbistep_kernel(tc, obs, emit_words, emit_scales, cum, step, 
             nc.vector.tensor_tensor(pair[:, part, :], s4[:, part, 0:2], s4[:, part, 2:4], MAX)
         got_scales = mid.tile([P, G], U8, name="got_scales", offset=0, align_bytes=64)
         nc.vector.tensor_copy(got_scales[:], scales[:].indirect(offs_sb[:]))
+        best_b = sb.tile([P, HG], F32, name="best_b")
+        nc.vector.tensor_tensor(best_b[:], pair[:, :, 0], pair[:, :, 1], MAX)
         obs_codes = sb.tile([P, Q], U32, name="obs_codes", align_bytes=64)
         obs_scales = sb.tile([P, Q], U8, name="obs_scales", align_bytes=64)
         nc.vector.quantize_mx(
@@ -144,8 +146,6 @@ def tile_attend_viterbistep_kernel(tc, obs, emit_words, emit_scales, cum, step, 
             )
             sums.append(emis)
 
-        best_b = late.tile([P, HG], F32, name="best_b", offset=G * 4)
-        nc.vector.tensor_tensor(best_b[:], pair[:, :, 0], pair[:, :, 1], MAX)
         best_a = sb.tile([P, HG], F32, name="best_a")
         nc.vector.tensor_reduce(best_a[:], up[:].rearrange("q n (g r) -> q (n g) r", r=2), mybir.AxisListType.X, MAX)
         bests = [best_b[:], best_a[:]]

@@ -27,7 +27,6 @@ HG = G // 2
 STRIPS = I // P
 PIECE = 2 * P
 PIECES = I // PIECE
-SPLIT = 2 * P
 BANK = 512
 
 
@@ -50,20 +49,30 @@ def tile_attend_viterbistep_kernel(tc, obs, emit_words, emit_scales, cum, step, 
         step_rows = shared.tile([P, PIECE], F32, name="step_rows", offset=0)
         ident = sb.tile([P, P], F32, name="ident")
 
-        nc.gpsimd.memset(scales[:].bitcast(I32), 0)
-        top = P - PIECES
+        plane = sb.tile([P, G], U8, name="plane", align_bytes=64)
+        row0 = P - D // QUADRANT
+        nc.gpsimd.memset(scales[0:row0, :].bitcast(I32), 0)
+        top = P // 2 - PIECES
+        end = P // 2
         nc.vector.memset(step_rows[0:top, :], 0.0)
+        nc.vector.memset(step_rows[end:P, :], 0.0)
+        nc.vector.memset(plane[:].bitcast(I32), 0)
 
+        nc.sync.dma_start(offs_sb[:], offs)
+        nc.scalar.dma_start(out=step_rows[top:end, :], in_=step[0].rearrange("(n j) -> n j", j=PIECE))
+        nc.sync.dma_start(out=scales[row0:P, :].bitcast(I32), in_=emit_scales[0].bitcast(I32))
         nc.sync.dma_start(offs2_sb[:], offs2)
-        nc.scalar.dma_start(out=step_rows[top:P, :], in_=step[0].rearrange("(n j) -> n j", j=PIECE))
         nc.sync.dma_start(out=cum_sb[:], in_=cum)
         nc.sync.dma_start(out=obs_sb[:], in_=obs.rearrange("(p j) q -> p j q", j=PACK))
-        nc.sync.dma_start(offs_sb[:], offs)
-        for j in range(PACK):
-            nc.sync.dma_start(
-                out=scales[j:P:QUADRANT, :].bitcast(I32), in_=emit_scales[0, j : D // QUADRANT : PACK, :].bitcast(I32)
-            )
         nc.sync.dma_start(out=words[:], in_=emit_words[0].rearrange("p n t -> p (n t)").bitcast(I32))
+
+        got_scales = sb.tile([P, G], U8, name="got_scales")
+        nc.vector.tensor_copy(got_scales[:], scales[:].indirect(offs_sb[:]))
+        for k in range(P // QUADRANT):
+            nc.sync.dma_start(
+                out=plane[QUADRANT * k : QUADRANT * k + PACK, :].bitcast(I32),
+                in_=got_scales[row0 + PACK * k : row0 + PACK * (k + 1), :].bitcast(I32),
+            )
 
         make_identity(nc, ident[:])
 
@@ -73,8 +82,8 @@ def tile_attend_viterbistep_kernel(tc, obs, emit_words, emit_scales, cum, step, 
         even_room = late.tile([P, 2 * P], F32, name="even_room", offset=0, align_bytes=64)
         spread_room = mid.tile([P, 16], F32, name="spread_room", offset=G - 32)
         odd = sb.tile([P, 2], F32, name="odd")
-        nc.scalar.activation(even_room[:, 0:PIECES], turned[:, 0, top:P], COPY)
-        nc.scalar.activation(spread_room[:, 0:2], turned[:, 1, top + 2 : P], COPY)
+        nc.scalar.activation(even_room[:, 0:PIECES], turned[:, 0, top:end], COPY)
+        nc.scalar.activation(spread_room[:, 0:2], turned[:, 1, top + 2 : end], COPY)
         nc.scalar.activation(odd[:], turned[:, 1, top : top + 2], COPY)
         spreads = []
         for n in range(2):
@@ -87,9 +96,9 @@ def tile_attend_viterbistep_kernel(tc, obs, emit_words, emit_scales, cum, step, 
             return offs2_sb[:, lo // LIST_ROWS : hi // LIST_ROWS]
 
         picked = shared.tile([P, I], F32, name="picked", offset=0)
-        for lo, hi in ((0, SPLIT), (I - P, I)):
+        for lo, hi in ((0, PIECE), (3 * PIECE, I)):
             nc.vector.tensor_copy(picked[:, lo:hi], cum_sb[:].indirect(entries(lo, hi)))
-        for lo, hi in ((2 * PIECE, 3 * PIECE), (3 * PIECE, I - P), (SPLIT, 2 * PIECE)):
+        for lo, hi in ((2 * PIECE, 3 * PIECE), (PIECE, 2 * PIECE)):
             nc.scalar.activation(picked[:, lo:hi], cum_sb[:].indirect(entries(lo, hi)), COPY)
 
         obs_bf = mid.tile([P, Q, PACK], BF16, name="obs_bf", offset=G, align_bytes=64)
@@ -106,8 +115,6 @@ def tile_attend_viterbistep_kernel(tc, obs, emit_words, emit_scales, cum, step, 
         pair = sb.tile([P, HG, 2], F32, name="pair")
         for part in (slice(0, HG // 2), slice(HG // 2, HG)):
             nc.vector.tensor_tensor(pair[:, part, :], s4[:, part, 0:2], s4[:, part, 2:4], MAX)
-        got_scales = mid.tile([P, G], U8, name="got_scales", offset=0, align_bytes=64)
-        nc.vector.tensor_copy(got_scales[:], scales[:].indirect(offs_sb[:]))
         best_b = sb.tile([P, HG], F32, name="best_b")
         nc.vector.tensor_tensor(best_b[:], pair[:, :, 0], pair[:, :, 1], MAX)
         obs_codes = sb.tile([P, Q], U32, name="obs_codes", align_bytes=64)
@@ -140,7 +147,7 @@ def tile_attend_viterbistep_kernel(tc, obs, emit_words, emit_scales, cum, step, 
                 lhsT=obs_codes[:].bitcast(FP8X4),
                 lhsT_scale=obs_scales[:],
                 rhs=got_words[:].bitcast(FP8X4),
-                rhs_scale=got_scales[:, (1 - h) * HG : (2 - h) * HG],
+                rhs_scale=plane[:, (1 - h) * HG : (2 - h) * HG],
                 start=True,
                 stop=True,
             )

@@ -27,6 +27,7 @@ HG = G // 2
 STRIPS = I // P
 PIECE = 2 * P
 PIECES = I // PIECE
+SPLIT = I - 192
 BANK = 512
 
 
@@ -62,7 +63,7 @@ def tile_attend_viterbistep_kernel(tc, obs, emit_words, emit_scales, cum, step, 
         nc.scalar.dma_start(out=step_rows[top:end, :], in_=step[0].rearrange("(n j) -> n j", j=PIECE))
         nc.sync.dma_start(out=scales[row0:P, :].bitcast(I32), in_=emit_scales[0].bitcast(I32))
         nc.sync.dma_start(offs2_sb[:], offs2)
-        nc.sync.dma_start(out=cum_sb[:], in_=cum)
+        nc.scalar.dma_start(out=cum_sb[:], in_=cum)
         nc.sync.dma_start(out=obs_sb[:], in_=obs.rearrange("(p j) q -> p j q", j=PACK))
         nc.sync.dma_start(out=words[:], in_=emit_words[0].rearrange("p n t -> p (n t)").bitcast(I32))
 
@@ -96,9 +97,9 @@ def tile_attend_viterbistep_kernel(tc, obs, emit_words, emit_scales, cum, step, 
             return offs2_sb[:, lo // LIST_ROWS : hi // LIST_ROWS]
 
         picked = shared.tile([P, I], F32, name="picked", offset=0)
-        for lo, hi in ((0, PIECE), (3 * PIECE, I)):
+        for lo, hi in ((0, PIECE), (SPLIT, I)):
             nc.vector.tensor_copy(picked[:, lo:hi], cum_sb[:].indirect(entries(lo, hi)))
-        for lo, hi in ((2 * PIECE, 3 * PIECE), (PIECE, 2 * PIECE)):
+        for lo, hi in ((2 * PIECE, SPLIT), (PIECE, 2 * PIECE)):
             nc.scalar.activation(picked[:, lo:hi], cum_sb[:].indirect(entries(lo, hi)), COPY)
 
         obs_bf = mid.tile([P, Q, PACK], BF16, name="obs_bf", offset=G, align_bytes=64)

@@ -28,6 +28,7 @@ STRIPS = I // P
 PIECE = 2 * P
 PIECES = I // PIECE
 SPLIT = I - 192
+LEAD = 384
 BANK = 512
 
 
@@ -59,11 +60,12 @@ def tile_attend_viterbistep_kernel(tc, obs, emit_words, emit_scales, cum, step, 
         nc.vector.memset(step_rows[end:P, :], 0.0)
         nc.vector.memset(plane[:].bitcast(I32), 0)
 
-        nc.sync.dma_start(offs_sb[:], offs)
-        nc.scalar.dma_start(out=step_rows[top:end, :], in_=step[0].rearrange("(n j) -> n j", j=PIECE))
         nc.sync.dma_start(out=scales[row0:P, :].bitcast(I32), in_=emit_scales[0].bitcast(I32))
+        nc.scalar.dma_start(out=step_rows[top:end, :], in_=step[0].rearrange("(n j) -> n j", j=PIECE))
+        nc.sync.dma_start(offs_sb[:], offs)
+        nc.sync.dma_start(out=cum_sb[:, 0:LEAD], in_=cum[:, 0:LEAD])
         nc.sync.dma_start(offs2_sb[:], offs2)
-        nc.scalar.dma_start(out=cum_sb[:], in_=cum)
+        nc.sync.dma_start(out=cum_sb[:, LEAD:U], in_=cum[:, LEAD:U])
         nc.sync.dma_start(out=obs_sb[:], in_=obs.rearrange("(p j) q -> p j q", j=PACK))
         nc.sync.dma_start(out=words[:], in_=emit_words[0].rearrange("p n t -> p (n t)").bitcast(I32))
 

@@ -27,7 +27,6 @@ HG = G // 2
 STRIPS = I // P
 PIECE = 2 * P
 PIECES = I // PIECE
-SPLIT = I - 192
 LEAD = 384
 BANK = 512
 
@@ -79,15 +78,13 @@ def tile_attend_viterbistep_kernel(tc, obs, emit_words, emit_scales, cum, step, 
 
         make_identity(nc, ident[:])
 
-        turned = ps_shared.tile([P, 2, BANK], F32, name="turned", offset=0)
+        turned = [ps_shared.tile([P, P], F32, name="turned0", offset=0), ps.tile([P, P], F32, name="turned1")]
         for e in range(2):
-            nc.tensor.transpose(turned[:, e, 0:P], step_rows[:, e:PIECE:2], ident[:])
+            nc.tensor.transpose(turned[e][:], step_rows[:, e:PIECE:2], ident[:])
         even_room = late.tile([P, 2 * P], F32, name="even_room", offset=0, align_bytes=64)
         spread_room = mid.tile([P, 16], F32, name="spread_room", offset=G - 32)
-        odd = sb.tile([P, 2], F32, name="odd")
-        nc.scalar.activation(even_room[:, 0:PIECES], turned[:, 0, top:end], COPY)
-        nc.scalar.activation(spread_room[:, 0:2], turned[:, 1, top + 2 : end], COPY)
-        nc.scalar.activation(odd[:], turned[:, 1, top : top + 2], COPY)
+        nc.scalar.activation(even_room[:, 0:PIECES], turned[0][:, top:end], COPY)
+        nc.scalar.activation(spread_room[:, 0:2], turned[1][:, top + 2 : end], COPY)
         spreads = []
         for n in range(2):
             spread = ps.tile([P, 2, P], F32, name="spread%d" % n)
@@ -99,9 +96,9 @@ def tile_attend_viterbistep_kernel(tc, obs, emit_words, emit_scales, cum, step, 
             return offs2_sb[:, lo // LIST_ROWS : hi // LIST_ROWS]
 
         picked = shared.tile([P, I], F32, name="picked", offset=0)
-        for lo, hi in ((0, PIECE), (SPLIT, I)):
+        for lo, hi in ((0, PIECE), (3 * PIECE, I)):
             nc.vector.tensor_copy(picked[:, lo:hi], cum_sb[:].indirect(entries(lo, hi)))
-        for lo, hi in ((2 * PIECE, SPLIT), (PIECE, 2 * PIECE)):
+        for lo, hi in ((2 * PIECE, 3 * PIECE), (PIECE, 2 * PIECE)):
             nc.scalar.activation(picked[:, lo:hi], cum_sb[:].indirect(entries(lo, hi)), COPY)
 
         obs_bf = mid.tile([P, Q, PACK], BF16, name="obs_bf", offset=G, align_bytes=64)
@@ -136,7 +133,7 @@ def tile_attend_viterbistep_kernel(tc, obs, emit_words, emit_scales, cum, step, 
             summed = shared.tile([P, P], F32, name="summed%d" % n, offset=(I + n * P) * 4)
             nc.scalar.activation(summed[:], down[:, 0, 0:P], IDENTITY, bias=even_room[:, n : n + 1])
             larger = shared.tile([P, P], F32, name="larger%d" % n, offset=(I + (2 + n) * P) * 4)
-            nc.vector.scalar_tensor_tensor(larger[:], down[:, 1, 0:P], odd[:, n : n + 1], summed[:], ADD, MAX)
+            nc.vector.scalar_tensor_tensor(larger[:], down[:, 1, 0:P], turned[1][:, top + n : top + n + 1], summed[:], ADD, MAX)
             nc.tensor.transpose(up[:, n, :], larger[:], ident[:])
 
         sums = []

@@ -27,7 +27,6 @@ HG = G // 2
 STRIPS = I // P
 PIECE = 2 * P
 PIECES = I // PIECE
-LEAD = 384
 BANK = 512
 
 
@@ -61,10 +60,10 @@ def tile_attend_viterbistep_kernel(tc, obs, emit_words, emit_scales, cum, step, 
 
         nc.sync.dma_start(out=scales[row0:P, :].bitcast(I32), in_=emit_scales[0].bitcast(I32))
         nc.scalar.dma_start(out=step_rows[top:end, :], in_=step[0].rearrange("(n j) -> n j", j=PIECE))
+        nc.scalar.dma_start(out=cum_sb[:, 0 : U // 2], in_=cum[:, 0 : U // 2])
         nc.sync.dma_start(offs_sb[:], offs)
-        nc.sync.dma_start(out=cum_sb[:, 0:LEAD], in_=cum[:, 0:LEAD])
         nc.sync.dma_start(offs2_sb[:], offs2)
-        nc.sync.dma_start(out=cum_sb[:, LEAD:U], in_=cum[:, LEAD:U])
+        nc.sync.dma_start(out=cum_sb[:, U // 2 : U], in_=cum[:, U // 2 : U])
         nc.sync.dma_start(out=obs_sb[:], in_=obs.rearrange("(p j) q -> p j q", j=PACK))
         nc.sync.dma_start(out=words[:], in_=emit_words[0].rearrange("p n t -> p (n t)").bitcast(I32))
 

@@ -35,21 +35,21 @@ def tile_attend_viterbistep_kernel(tc, obs, emit_words, emit_scales, cum, step, 
     with ExitStack() as ctx:
         sb = ctx.enter_context(tc.tile_pool(name="sb", bufs=1))
         shared = ctx.enter_context(tc.tile_pool(name="shared", bufs=1))
-        ps = ctx.enter_context(tc.psum_pool(name="ps", bufs=1))
-
-        ps_shared = ctx.enter_context(tc.psum_pool(name="ps_shared", bufs=1))
-        mid = ctx.enter_context(tc.tile_pool(name="mid", bufs=1))
         late = ctx.enter_context(tc.tile_pool(name="late", bufs=1))
+        ps = ctx.enter_context(tc.psum_pool(name="ps", bufs=1))
+        ps_shared = ctx.enter_context(tc.psum_pool(name="ps_shared", bufs=1))
+
         cum_sb = sb.tile([P, U], F32, name="cum_sb")
         offs2_sb = sb.tile([P, I // LIST_ROWS], U16, name="offs2_sb")
         offs_sb = sb.tile([P, G // LIST_ROWS], U16, name="offs_sb")
-        obs_sb = shared.tile([P, PACK, Q], F32, name="obs_sb", offset=I * 4)
+        obs_sb = sb.tile([P, PACK, Q], F32, name="obs_sb")
         words = sb.tile([P, T], I32, name="words")
         scales = sb.tile([P, T], U8, name="scales")
-        step_rows = shared.tile([P, PIECE], F32, name="step_rows", offset=0)
+        step_room = shared.tile([P, I + P], F32, name="step_room", offset=0)
+        step_rows = step_room[:, 0:PIECE]
         ident = sb.tile([P, P], F32, name="ident")
-
         plane = sb.tile([P, G], U8, name="plane", align_bytes=64)
+
         row0 = P - D // QUADRANT
         nc.gpsimd.memset(scales[0:row0, :].bitcast(I32), 0)
         top = P // 2 - PIECES
@@ -77,86 +77,85 @@ def tile_attend_viterbistep_kernel(tc, obs, emit_words, emit_scales, cum, step, 
 
         make_identity(nc, ident[:])
 
-        turned = [ps_shared.tile([P, P], F32, name="turned0", offset=0), ps.tile([P, P], F32, name="turned1")]
-        for e in range(2):
-            nc.tensor.transpose(turned[e][:], step_rows[:, e:PIECE:2], ident[:])
-        even_room = late.tile([P, 2 * P], F32, name="even_room", offset=0, align_bytes=64)
-        spread_room = mid.tile([P, 16], F32, name="spread_room", offset=G - 32)
-        nc.scalar.activation(even_room[:, 0:PIECES], turned[0][:, top:end], COPY)
-        nc.scalar.activation(spread_room[:, 0:2], turned[1][:, top + 2 : end], COPY)
-        spreads = []
-        for n in range(2):
-            spread = ps.tile([P, 2, P], F32, name="spread%d" % n)
-            for e, column in enumerate((even_room[:, 2 + n : 3 + n], spread_room[:, n : n + 1])):
-                nc.tensor.transpose(spread[:, e, :], column.to_broadcast([P, P]), ident[:])
-            spreads.append(spread[:].rearrange("q e p -> q p e"))
+        step_even = ps_shared.tile([P, P], F32, name="step_even", offset=3 * BANK * 4)
+        step_odd = ps.tile([P, P], F32, name="step_odd")
+        for e, turned in enumerate((step_even, step_odd)):
+            nc.tensor.transpose(turned[:], step_rows[:, e:PIECE:2], ident[:])
+        even_room = sb.tile([P, PIECES], F32, name="even_room")
+        nc.scalar.activation(even_room[:, 0:PIECES], step_even[:, top:end], COPY)
 
-        def entries(lo, hi):
-            return offs2_sb[:, lo // LIST_ROWS : hi // LIST_ROWS]
+        picked = []
+        for n in range(PIECES):
+            piece_tile = shared.tile([P, PIECE], F32, name="picked%d" % n, offset=n * PIECE * 4)
+            picked.append(piece_tile)
+            piece = piece_tile[:]
+            first = n * PIECE // LIST_ROWS
+            half = P // LIST_ROWS
+            nc.vector.tensor_copy(piece[:, 0:P], cum_sb[:].indirect(offs2_sb[:, first : first + half]))
+            nc.scalar.activation(piece[:, P:PIECE], cum_sb[:].indirect(offs2_sb[:, first + half : first + 2 * half]), COPY)
 
-        picked = shared.tile([P, I], F32, name="picked", offset=0)
-        for lo, hi in ((0, PIECE), (3 * PIECE, I)):
-            nc.vector.tensor_copy(picked[:, lo:hi], cum_sb[:].indirect(entries(lo, hi)))
-        for lo, hi in ((2 * PIECE, 3 * PIECE), (PIECE, 2 * PIECE)):
-            nc.scalar.activation(picked[:, lo:hi], cum_sb[:].indirect(entries(lo, hi)), COPY)
+        downs = []
+        for n in range(PIECES - 1):
+            down = ps_shared.tile([P, 2, P], F32, name="down%d" % n, offset=n * BANK * 4)
+            downs.append((down[:, 0, :], down[:, 1, :]))
+        even_last = ps_shared.tile([P, P], F32, name="even_last", offset=3 * BANK * 4)
+        odd_last = ps.tile([P, P], F32, name="odd_last")
+        downs.append((even_last[:], odd_last[:]))
+        for n, down in enumerate(downs):
+            for e in range(2):
+                nc.tensor.transpose(down[e], picked[n][:, e:PIECE:2], ident[:])
 
-        obs_bf = mid.tile([P, Q, PACK], BF16, name="obs_bf", offset=G, align_bytes=64)
-        nc.scalar.copy(
+        obs_bf = shared.tile([P, Q, PACK], BF16, name="obs_bf", offset=I * 4, align_bytes=64)
+        nc.vector.tensor_copy(
             obs_bf[:].rearrange("p (c i) j -> p c j i", i=4),
             obs_sb[:].rearrange("p j (c i) -> p c j i", i=4),
         )
-
-        s = sb.tile([P, 2, P, 2], F32, name="s")
-        for n in range(2):
-            piece = picked[:, (2 + n) * PIECE : (3 + n) * PIECE].rearrange("q (p e) -> q p e", e=2)
-            nc.vector.tensor_tensor(s[:, n, :, :], piece, spreads[n], ADD)
-        s4 = s[:].rearrange("q n (g x) e -> q (n g) (x e)", x=2)
-        pair = sb.tile([P, HG, 2], F32, name="pair")
-        for part in (slice(0, HG // 2), slice(HG // 2, HG)):
-            nc.vector.tensor_tensor(pair[:, part, :], s4[:, part, 0:2], s4[:, part, 2:4], MAX)
-        best_b = sb.tile([P, HG], F32, name="best_b")
-        nc.vector.tensor_tensor(best_b[:], pair[:, :, 0], pair[:, :, 1], MAX)
         obs_codes = sb.tile([P, Q], U32, name="obs_codes", align_bytes=64)
         obs_scales = sb.tile([P, Q], U8, name="obs_scales", align_bytes=64)
-        nc.vector.quantize_mx(
-            out=obs_codes[:].bitcast(FP8X4), scales=obs_scales[:], in_=obs_bf[:].rearrange("p q j -> p (q j)")
-        )
 
-        down_a = ps_shared.tile([P, 2, P], F32, name="down_a", offset=0)
-        down_b = ps_shared.tile([P, 2, BANK], F32, name="down_b", offset=BANK * 4)
-        up = ps.tile([P, 2, P], F32, name="up")
-        for n, down in enumerate((down_a, down_b)):
-            for e in range(2):
-                nc.tensor.transpose(down[:, e, 0:P], picked[:, n * PIECE + e : (n + 1) * PIECE : 2], ident[:])
-        for n, down in enumerate((down_a, down_b)):
-            summed = shared.tile([P, P], F32, name="summed%d" % n, offset=(I + n * P) * 4)
-            nc.scalar.activation(summed[:], down[:, 0, 0:P], IDENTITY, bias=even_room[:, n : n + 1])
-            larger = shared.tile([P, P], F32, name="larger%d" % n, offset=(I + (2 + n) * P) * 4)
-            nc.vector.scalar_tensor_tensor(larger[:], down[:, 1, 0:P], turned[1][:, top + n : top + n + 1], summed[:], ADD, MAX)
-            nc.tensor.transpose(up[:, n, :], larger[:], ident[:])
+        ups = [ps.tile([P, 2, P], F32, name="up%d" % h) for h in range(2)]
+        for n, down in enumerate(downs):
+            summed_room = late.tile([P, 2 * P], F32, name="summed%d" % n, offset=((PIECES - 2 - n) % PIECES) * 2 * P * 4, align_bytes=64)
+            summed = summed_room[:, 0:P]
+            nc.scalar.activation(summed, down[0], IDENTITY, bias=even_room[:, n : n + 1])
+            larger = sb.tile([P, P], F32, name="larger%d" % n)
+            nc.vector.scalar_tensor_tensor(larger[:], down[1], step_odd[:, top + n : top + n + 1], summed, ADD, MAX)
+            nc.tensor.transpose(ups[n // 2][:, n % 2, :], larger[:], ident[:])
+            if n == 0:
+                nc.vector.quantize_mx(
+                    out=obs_codes[:].bitcast(FP8X4), scales=obs_scales[:], in_=obs_bf[:].rearrange("p q j -> p (q j)")
+                )
 
         sums = []
         for h in range(2):
             got_words = late.tile([P, HG], U32, name="got_words%d" % h, offset=h * HG * 4, align_bytes=64)
-            listed = offs_sb[:, (1 - h) * HG // LIST_ROWS : (2 - h) * HG // LIST_ROWS]
+            listed = offs_sb[:, h * HG // LIST_ROWS : (h + 1) * HG // LIST_ROWS]
             nc.vector.tensor_copy(got_words[:], words[:].bitcast(U32).indirect(listed))
-            emis = ps_shared.tile([P, HG], F32, name="emis%d" % h, offset=(1 + h) * BANK * 4)
+            emis = ps_shared.tile([P, HG], F32, name="emis%d" % h, offset=h * BANK * 4)
             nc.tensor.matmul_mx(
                 out=emis[:],
                 lhsT=obs_codes[:].bitcast(FP8X4),
                 lhsT_scale=obs_scales[:],
                 rhs=got_words[:].bitcast(FP8X4),
-                rhs_scale=plane[:, (1 - h) * HG : (2 - h) * HG],
+                rhs_scale=plane[:, h * HG : (h + 1) * HG],
                 start=True,
                 stop=True,
             )
             sums.append(emis)
 
-        best_a = sb.tile([P, HG], F32, name="best_a")
-        nc.vector.tensor_reduce(best_a[:], up[:].rearrange("q n (g r) -> q (n g) r", r=2), mybir.AxisListType.X, MAX)
-        bests = [best_b[:], best_a[:]]
+        bests = []
+        for h in range(2):
+            best = late.tile([P, HG], F32, name="best%d" % h, offset=(3 * 2 + h) * P * 4, align_bytes=64)
+            pairs = ups[h][:].rearrange("q n (g r) -> q (n g) r", r=2)
+            if h == 0:
+                second = sb.tile([P, HG], F32, name="second")
+                nc.scalar.activation(second[:], pairs[:, :, 1], COPY)
+                nc.vector.tensor_tensor(best[:], pairs[:, :, 0], second[:], MAX)
+            else:
+                nc.vector.tensor_reduce(best[:], pairs, mybir.AxisListType.X, MAX)
+            bests.append(best)
 
         for h, queue in ((0, nc.scalar), (1, nc.sync)):
-            res = shared.tile([P, HG], F32, name="res%d" % h, offset=(I + (3 + h) * P) * 4)
-            nc.vector.tensor_tensor(res[:], sums[h][:], bests[h], ADD)
-            queue.dma_start(out=out[:, (1 - h) * HG : (2 - h) * HG], in_=res[:])
+            res = sb.tile([P, HG], F32, name="res%d" % h)
+            nc.vector.tensor_tensor(res[:], sums[h][:], bests[h][:], ADD)
+            queue.dma_start(out=out[:, h * HG : (h + 1) * HG], in_=res[:])

@@ -58,12 +58,13 @@ def tile_attend_viterbistep_kernel(tc, obs, emit_words, emit_scales, cum, step, 
         nc.vector.memset(step_rows[end:P, :], 0.0)
         nc.vector.memset(plane[:].bitcast(I32), 0)
 
+        cut = 5 * U // 8
+        nc.scalar.dma_start(out=cum_sb[:, 0:cut], in_=cum[:, 0:cut])
+        nc.sync.dma_start(out=step_rows[top:end, :], in_=step[0].rearrange("(n j) -> n j", j=PIECE))
         nc.sync.dma_start(out=scales[row0:P, :].bitcast(I32), in_=emit_scales[0].bitcast(I32))
-        nc.scalar.dma_start(out=step_rows[top:end, :], in_=step[0].rearrange("(n j) -> n j", j=PIECE))
-        nc.scalar.dma_start(out=cum_sb[:, 0 : U // 2], in_=cum[:, 0 : U // 2])
         nc.sync.dma_start(offs_sb[:], offs)
         nc.sync.dma_start(offs2_sb[:], offs2)
-        nc.sync.dma_start(out=cum_sb[:, U // 2 : U], in_=cum[:, U // 2 : U])
+        nc.sync.dma_start(out=cum_sb[:, cut:U], in_=cum[:, cut:U])
         nc.sync.dma_start(out=obs_sb[:], in_=obs.rearrange("(p j) q -> p j q", j=PACK))
         nc.sync.dma_start(out=words[:], in_=emit_words[0].rearrange("p n t -> p (n t)").bitcast(I32))
 

@@ -50,8 +50,9 @@ def tile_attend_viterbistep_kernel(tc, obs, emit_words, emit_scales, cum, step, 
         ident = sb.tile([P, P], F32, name="ident")
         plane = sb.tile([P, G], U8, name="plane", align_bytes=64)
 
-        row0 = P - D // QUADRANT
-        nc.gpsimd.memset(scales[0:row0, :].bitcast(I32), 0)
+        row0 = QUADRANT
+        row_end = row0 + PACK * (D // QUADRANT)
+        nc.gpsimd.memset(scales[:].bitcast(I32), 0)
         top = P // 2 - PIECES
         end = P // 2
         nc.vector.memset(step_rows[0:top, :], 0.0)
@@ -61,8 +62,8 @@ def tile_attend_viterbistep_kernel(tc, obs, emit_words, emit_scales, cum, step, 
         cut = 5 * U // 8
         nc.scalar.dma_start(out=cum_sb[:, 0:cut], in_=cum[:, 0:cut])
         nc.sync.dma_start(out=step_rows[top:end, :], in_=step[0].rearrange("(n j) -> n j", j=PIECE))
-        nc.sync.dma_start(out=scales[row0:P, :].bitcast(I32), in_=emit_scales[0].bitcast(I32))
         nc.sync.dma_start(offs_sb[:], offs)
+        nc.sync.dma_start(out=scales[row0:row_end:PACK, :].bitcast(I32), in_=emit_scales[0].bitcast(I32))
         nc.sync.dma_start(offs2_sb[:], offs2)
         nc.sync.dma_start(out=cum_sb[:, cut:U], in_=cum[:, cut:U])
         nc.sync.dma_start(out=obs_sb[:], in_=obs.rearrange("(p j) q -> p j q", j=PACK))
@@ -73,7 +74,7 @@ def tile_attend_viterbistep_kernel(tc, obs, emit_words, emit_scales, cum, step, 
         for k in range(P // QUADRANT):
             nc.sync.dma_start(
                 out=plane[QUADRANT * k : QUADRANT * k + PACK, :].bitcast(I32),
-                in_=got_scales[row0 + PACK * k : row0 + PACK * (k + 1), :].bitcast(I32),
+                in_=got_scales[row0 + PACK * PACK * k : row0 + PACK * PACK * (k + 1) : PACK, :].bitcast(I32),
             )
 
         make_identity(nc, ident[:])

from contextlib import ExitStack

import concourse.mybir as mybir
from concourse.masks import make_identity

D, T, G, U, I, Q = 512, 2048, 256, 1024, 1024, 128
FLOPS = 2 * D * Q * G

F32 = mybir.dt.float32
BF16 = mybir.dt.bfloat16
I32 = mybir.dt.int32
U32 = mybir.dt.uint32
U16 = mybir.dt.uint16
U8 = mybir.dt.uint8
FP8X4 = mybir.dt.float8_e4m3fn_x4
ADD = mybir.AluOpType.add
MAX = mybir.AluOpType.max
IDENTITY = mybir.ActivationFunctionType.Identity
COPY = mybir.ActivationFunctionType.Copy

P = 128
PACK = 4
QUADRANT = 32
LIST_ROWS = 16
R = I // G
HG = G // 2
STRIPS = I // P
PIECE = 2 * P
PIECES = I // PIECE
BANK = 512


def tile_attend_viterbistep_kernel(tc, obs, emit_words, emit_scales, cum, step, offs, offs2, out):
    nc = tc.nc
    with ExitStack() as ctx:
        sb = ctx.enter_context(tc.tile_pool(name="sb", bufs=1))
        shared = ctx.enter_context(tc.tile_pool(name="shared", bufs=1))
        late = ctx.enter_context(tc.tile_pool(name="late", bufs=1))
        ps = ctx.enter_context(tc.psum_pool(name="ps", bufs=1))
        ps_shared = ctx.enter_context(tc.psum_pool(name="ps_shared", bufs=1))

        cum_sb = sb.tile([P, U], F32, name="cum_sb")
        offs2_sb = sb.tile([P, I // LIST_ROWS], U16, name="offs2_sb")
        offs_sb = sb.tile([P, G // LIST_ROWS], U16, name="offs_sb")
        obs_sb = sb.tile([P, PACK, Q], F32, name="obs_sb")
        words = sb.tile([P, T], I32, name="words")
        scales = sb.tile([P, T], U8, name="scales")
        step_room = shared.tile([P, I + P], F32, name="step_room", offset=0)
        step_rows = step_room[:, 0:PIECE]
        ident = sb.tile([P, P], F32, name="ident")
        plane = sb.tile([P, G], U8, name="plane", align_bytes=64)

        row0 = QUADRANT
        row_end = row0 + PACK * (D // QUADRANT)
        nc.gpsimd.memset(scales[:].bitcast(I32), 0)
        top = P // 2 - PIECES
        end = P // 2
        nc.vector.memset(step_rows[0:top, :], 0.0)
        nc.vector.memset(step_rows[end:P, :], 0.0)
        nc.vector.memset(plane[:].bitcast(I32), 0)

        cut = 5 * U // 8
        nc.scalar.dma_start(out=cum_sb[:, 0:cut], in_=cum[:, 0:cut])
        nc.sync.dma_start(out=step_rows[top:end, :], in_=step[0].rearrange("(n j) -> n j", j=PIECE))
        nc.sync.dma_start(offs_sb[:], offs)
        nc.sync.dma_start(out=scales[row0:row_end:PACK, :].bitcast(I32), in_=emit_scales[0].bitcast(I32))
        nc.sync.dma_start(offs2_sb[:], offs2)
        nc.sync.dma_start(out=cum_sb[:, cut:U], in_=cum[:, cut:U])
        nc.sync.dma_start(out=obs_sb[:], in_=obs.rearrange("(p j) q -> p j q", j=PACK))
        nc.sync.dma_start(out=words[:], in_=emit_words[0].rearrange("p n t -> p (n t)").bitcast(I32))

        got_scales = sb.tile([P, G], U8, name="got_scales")
        nc.vector.tensor_copy(got_scales[:], scales[:].indirect(offs_sb[:]))
        for k in range(P // QUADRANT):
            nc.sync.dma_start(
                out=plane[QUADRANT * k : QUADRANT * k + PACK, :].bitcast(I32),
                in_=got_scales[row0 + PACK * PACK * k : row0 + PACK * PACK * (k + 1) : PACK, :].bitcast(I32),
            )

        make_identity(nc, ident[:])

        step_even = ps_shared.tile([P, P], F32, name="step_even", offset=3 * BANK * 4)
        step_odd = ps.tile([P, P], F32, name="step_odd")
        for e, turned in enumerate((step_even, step_odd)):
            nc.tensor.transpose(turned[:], step_rows[:, e:PIECE:2], ident[:])
        even_room = sb.tile([P, PIECES], F32, name="even_room")
        nc.scalar.activation(even_room[:, 0:PIECES], step_even[:, top:end], COPY)

        picked = []
        for n in range(PIECES):
            piece_tile = shared.tile([P, PIECE], F32, name="picked%d" % n, offset=n * PIECE * 4)
            picked.append(piece_tile)
            piece = piece_tile[:]
            first = n * PIECE // LIST_ROWS
            half = P // LIST_ROWS
            nc.vector.tensor_copy(piece[:, 0:P], cum_sb[:].indirect(offs2_sb[:, first : first + half]))
            nc.scalar.activation(piece[:, P:PIECE], cum_sb[:].indirect(offs2_sb[:, first + half : first + 2 * half]), COPY)

        downs = []
        for n in range(PIECES - 1):
            down = ps_shared.tile([P, 2, P], F32, name="down%d" % n, offset=n * BANK * 4)
            downs.append((down[:, 0, :], down[:, 1, :]))
        even_last = ps_shared.tile([P, P], F32, name="even_last", offset=3 * BANK * 4)
        odd_last = ps.tile([P, P], F32, name="odd_last")
        downs.append((even_last[:], odd_last[:]))
        for n, down in enumerate(downs):
            for e in range(2):
                nc.tensor.transpose(down[e], picked[n][:, e:PIECE:2], ident[:])

        obs_bf = shared.tile([P, Q, PACK], BF16, name="obs_bf", offset=I * 4, align_bytes=64)
        nc.vector.tensor_copy(
            obs_bf[:].rearrange("p (c i) j -> p c j i", i=4),
            obs_sb[:].rearrange("p j (c i) -> p c j i", i=4),
        )
        obs_codes = sb.tile([P, Q], U32, name="obs_codes", align_bytes=64)
        obs_scales = sb.tile([P, Q], U8, name="obs_scales", align_bytes=64)

        ups = [ps.tile([P, 2, P], F32, name="up%d" % h) for h in range(2)]
        for n, down in enumerate(downs):
            summed_room = late.tile([P, 2 * P], F32, name="summed%d" % n, offset=((PIECES - 2 - n) % PIECES) * 2 * P * 4, align_bytes=64)
            summed = summed_room[:, 0:P]
            nc.scalar.activation(summed, down[0], IDENTITY, bias=even_room[:, n : n + 1])
            larger = sb.tile([P, P], F32, name="larger%d" % n)
            nc.vector.scalar_tensor_tensor(larger[:], down[1], step_odd[:, top + n : top + n + 1], summed, ADD, MAX)
            nc.tensor.transpose(ups[n // 2][:, n % 2, :], larger[:], ident[:])
            if n == 0:
                nc.vector.quantize_mx(
                    out=obs_codes[:].bitcast(FP8X4), scales=obs_scales[:], in_=obs_bf[:].rearrange("p q j -> p (q j)")
                )

        sums = []
        for h in range(2):
            got_words = late.tile([P, HG], U32, name="got_words%d" % h, offset=h * HG * 4, align_bytes=64)
            listed = offs_sb[:, h * HG // LIST_ROWS : (h + 1) * HG // LIST_ROWS]
            nc.vector.tensor_copy(got_words[:], words[:].bitcast(U32).indirect(listed))
            emis = ps_shared.tile([P, HG], F32, name="emis%d" % h, offset=h * BANK * 4)
            nc.tensor.matmul_mx(
                out=emis[:],
                lhsT=obs_codes[:].bitcast(FP8X4),
                lhsT_scale=obs_scales[:],
                rhs=got_words[:].bitcast(FP8X4),
                rhs_scale=plane[:, h * HG : (h + 1) * HG],
                start=True,
                stop=True,
            )
            sums.append(emis)

        bests = []
        for h in range(2):
            best = late.tile([P, HG], F32, name="best%d" % h, offset=(3 * 2 + h) * P * 4, align_bytes=64)
            pairs = ups[h][:].rearrange("q n (g r) -> q (n g) r", r=2)
            if h == 0:
                second = sb.tile([P, HG], F32, name="second")
                nc.scalar.activation(second[:], pairs[:, :, 1], COPY)
                nc.vector.tensor_tensor(best[:], pairs[:, :, 0], second[:], MAX)
            else:
                nc.vector.tensor_reduce(best[:], pairs, mybir.AxisListType.X, MAX)
            bests.append(best)

        for h, queue in ((0, nc.scalar), (1, nc.sync)):
            res = sb.tile([P, HG], F32, name="res%d" % h)
            nc.vector.tensor_tensor(res[:], sums[h][:], bests[h][:], ADD)
            queue.dma_start(out=out[:, h * HG : (h + 1) * HG], in_=res[:])
